import numpy as np
import ml_dtypes


def mxq(x, axis, fmt="e4m3"):
    dtype, down = {"e4m3": (ml_dtypes.float8_e4m3fn, 7), "e5m2": (ml_dtypes.float8_e5m2, 14)}[fmt]
    v = np.moveaxis(np.asarray(x, np.float32).astype(ml_dtypes.bfloat16).astype(np.float64), axis, -1)
    blocks = v.reshape(v.shape[:-1] + (-1, 32))
    amax = np.abs(blocks).max(-1, keepdims=True)
    byte = np.maximum(np.where(amax > 0, np.frexp(amax)[1] - 1 + 127, 0) - down, 1)
    scale = np.exp2(byte - 127.0)
    codes = (blocks / scale).astype(np.float32).astype(dtype).astype(np.float64)
    return np.moveaxis((codes * scale).reshape(v.shape), -1, axis)


WIDE = False


def mx_kscale(k):
    if not WIDE:
        return np.ones(k)
    levels = np.array([10, -10, 5, -5, 0])
    if k % 512:
        return np.exp2(np.random.permutation(np.resize(levels, k // 32))).repeat(32)
    a = np.empty((k // 512, 16))
    for p in range(k // 512):
        a[p, :8] = np.random.permutation(np.resize(levels, 8))
        for g in range(8):
            far = levels[np.abs(levels - a[p, g]) >= 10]
            a[p, g + 8] = far[np.random.randint(len(far))]
    return np.exp2(a.ravel()).repeat(32)


def f64(x):
    return np.asarray(x).astype(np.float64)


def striped(idx):
    return np.tile(idx.reshape(-1, 16).T, (8, 1)).astype(np.uint16)


def unstriped(offs):
    return offs[:16].T.reshape(-1).astype(np.int64)


def pack_weight(w):
    k, n = w.shape
    w = f64(np.asarray(w, np.float32).astype(ml_dtypes.bfloat16)).reshape(k // 32, 32, n)
    amax = np.abs(w).max(1)
    byte = np.clip(np.where(amax > 0, np.frexp(amax)[1] - 1 + 127 - 7, 1), 1, 254)
    scaled = (w * np.exp2(127.0 - byte)[:, None, :]).reshape(k, n).astype(np.float32)
    words = np.ascontiguousarray(scaled.reshape(k // 512, 128, 4, n).transpose(0, 1, 3, 2)).astype(ml_dtypes.float8_e4m3fn).view(np.uint8)
    return words, np.ascontiguousarray(byte.astype(np.uint8).reshape(k // 512, 16, n))


def unpack_weight(words, scales):
    g, p, n, _ = words.shape
    vals = np.ascontiguousarray(words).view(ml_dtypes.float8_e4m3fn).astype(np.float64) * np.repeat(np.exp2(scales.astype(np.float64) - 127.0), 8, axis=1)[..., None]
    return vals.transpose(0, 1, 3, 2).reshape(g * 512, n)


K, T, D, S, V, N = 1024, 2048, 2, 1280, 640, 256


def setup_inputs():
    n = np.random.standard_normal
    s = mx_kscale(K)[:, None]
    packed = pack_weight(n((K, T)) * s)
    return {
        "x_words": packed[0],
        "x_scales": packed[1],
        "w": (n((D, K, N)) / np.sqrt(K) / s[None]).astype(np.float32),
        "offs": striped(np.random.permutation(T)[:S]),
    }


def reference(x_words, x_scales, w, offs):
    idx = unstriped(offs)
    xq = unpack_weight(x_words, x_scales)[:, idx]
    wq = mxq(f64(w), 1, "e4m3")
    y0 = wq[0].T @ xq[:, :V]
    y1 = wq[1].T @ xq[:, V:]
    return y0 * y1

@@ -1,0 +1,137 @@
+from contextlib import ExitStack
+
+import concourse.mybir as mybir
+
+K, T, D, S, V, N = 1024, 2048, 2, 1280, 640, 256
+FLOPS = 2 * K * N * S + N * V
+
+F32 = mybir.dt.float32
+BF16 = mybir.dt.bfloat16
+I32 = mybir.dt.int32
+U32 = mybir.dt.uint32
+U16 = mybir.dt.uint16
+U8 = mybir.dt.uint8
+FP8X4 = mybir.dt.float8_e4m3fn_x4
+
+P = 128
+PACK = 4
+K_PASS = P * PACK
+PASSES = K // K_PASS
+M_TILES = N // P
+QUAD = 32
+ROWS0 = 96
+CHUNKS = ((0, 512), (512, 640))
+
+
+def tile_picked_pair_lin_mul_sub_p_kernel(tc, x_words, x_scales, w, offs, out):
+    nc = tc.nc
+    with ExitStack() as ctx:
+        keep = ctx.enter_context(tc.tile_pool(name="keep", bufs=1))
+        psum = ctx.enter_context(tc.psum_pool(name="psum", bufs=1))
+
+        offsets = keep.tile([P, S // 16], U16, name="offsets")
+        byte_table = keep.tile([P, T], U8, name="byte_table", align_bytes=64)
+        byte_picked = keep.tile([P, S], U8, name="byte_picked", align_bytes=64)
+        x_plane = keep.tile([P, S], U8, name="x_plane", align_bytes=64)
+        word_table = [keep.tile([P, T], U32, name="word_table%d" % o, align_bytes=64) for o in range(PASSES)]
+        w_raw = {}
+        for d in range(D):
+            for o in range(PASSES):
+                w_raw[d, o] = keep.tile([P, PACK, N], F32, name="w_raw%d%d" % (d, o), align_bytes=64)
+
+        def load_words(o):
+            nc.sync.dma_start(out=word_table[o][:].bitcast(I32),
+                              in_=x_words[o].rearrange("p n t -> p (n t)").bitcast(I32))
+
+        def load_w(d, o):
+            nc.sync.dma_start(out=w_raw[d, o][:],
+                              in_=w[d, o * K_PASS:(o + 1) * K_PASS, :].rearrange("(p j) m -> p j m", j=PACK))
+
+        nc.vector.memset(byte_table[0:ROWS0, :].bitcast(I32), 0)
+        nc.gpsimd.memset(x_plane[:].bitcast(I32), 0)
+        nc.sync.dma_start(offsets[:], offs)
+        for o in range(PASSES):
+            nc.sync.dma_start(out=byte_table[ROWS0 + 16 * o:ROWS0 + 16 * (o + 1), :].bitcast(I32),
+                              in_=x_scales[o].rearrange("(q j) c -> j q c", j=4).bitcast(I32))
+        load_words(0)
+        load_w(0, 0)
+        load_words(1)
+        load_w(0, 1)
+        load_w(1, 0)
+        load_w(1, 1)
+
+        nc.vector.tensor_copy(byte_picked[:], byte_table[:].indirect(offsets[:]))
+        for q in range(4):
+            nc.scalar.dma_start(out=x_plane[QUAD * q:QUAD * q + 8, :].bitcast(I32),
+                                in_=byte_picked[ROWS0 + q:P:4, :].bitcast(I32))
+
+        x_codes = {}
+
+        def gather_words(d, o):
+            x_codes[d, o] = keep.tile([P, V], U32, name="x_codes%d%d" % (d, o), align_bytes=64)
+            cols = slice(d * V // 16, (d + 1) * V // 16)
+            nc.vector.tensor_copy(x_codes[d, o][:], word_table[o][:].indirect(offsets[:, cols]))
+
+        w_bf = {}
+        w_codes = {}
+        w_scales = {}
+
+        def cast_w(d, o, mt, copy):
+            w_bf[d, o, mt] = keep.tile([P, P * PACK], BF16, name="w_bf%d%d%d" % (d, o, mt), align_bytes=64)
+            copy(w_bf[d, o, mt][:].rearrange("p (c i j) -> p c j i", i=4, j=PACK),
+                 w_raw[d, o][:, :, mt * P:(mt + 1) * P].rearrange("p j (c i) -> p c j i", i=4))
+
+        def quantize_w(d, o, mt):
+            w_codes[d, o, mt] = keep.tile([P, P], U32, name="w_codes%d%d%d" % (d, o, mt), align_bytes=64)
+            w_scales[d, o, mt] = keep.tile([P, P], U8, name="w_scales%d%d%d" % (d, o, mt), align_bytes=64)
+            nc.vector.quantize_mx(out=w_codes[d, o, mt][:].bitcast(FP8X4), scales=w_scales[d, o, mt][:],
+                                  in_=w_bf[d, o, mt][:])
+
+        acc = {}
+        for d in range(D):
+            for mt in range(M_TILES):
+                for a, b in CHUNKS:
+                    acc[d, mt, a] = psum.tile([P, b - a], F32, name="acc%d%d_%d" % (d, mt, a))
+
+        def multiply(d, o, mt):
+            for a, b in CHUNKS:
+                nc.tensor.matmul_mx(out=acc[d, mt, a][:],
+                                    lhsT=w_codes[d, o, mt][:].bitcast(FP8X4), lhsT_scale=w_scales[d, o, mt][:],
+                                    rhs=x_codes[d, o][:, a:b].bitcast(FP8X4),
+                                    rhs_scale=x_plane[4 * o:P, d * V + a:d * V + b],
+                                    start=(o == 0), stop=(o == PASSES - 1))
+
+        gather_words(0, 0)
+        gather_words(1, 0)
+        for mt in range(M_TILES):
+            cast_w(0, 0, mt, nc.scalar.copy)
+        for mt in range(M_TILES):
+            quantize_w(0, 0, mt)
+            multiply(0, 0, mt)
+        gather_words(0, 1)
+        gather_words(1, 1)
+        for mt in range(M_TILES):
+            cast_w(0, 1, mt, nc.scalar.copy)
+        for mt in range(M_TILES):
+            quantize_w(0, 1, mt)
+            multiply(0, 1, mt)
+        for mt in range(M_TILES):
+            cast_w(1, 0, mt, nc.scalar.copy)
+        for mt in range(M_TILES):
+            cast_w(1, 1, mt, nc.vector.tensor_copy)
+        for mt in range(M_TILES):
+            for o in range(PASSES):
+                quantize_w(1, o, mt)
+                multiply(1, o, mt)
+
+        y0 = {}
+        for mt in range(M_TILES):
+            for a, b in CHUNKS:
+                y0[mt, a] = keep.tile([P, b - a], F32, name="y0_%d_%d" % (mt, a), align_bytes=64)
+                nc.scalar.copy(y0[mt, a][:], acc[0, mt, a][:])
+        for mt in range(M_TILES):
+            for a, b in CHUNKS:
+                res = keep.tile([P, b - a], F32, name="res%d_%d" % (mt, a), align_bytes=64)
+                nc.vector.tensor_tensor(res[:], acc[1, mt, a][:], y0[mt, a][:], mybir.AluOpType.mult)
+                queue = nc.sync if a == 0 else nc.scalar
+                queue.dma_start(out=out[mt * P:(mt + 1) * P, a:b], in_=res[:])

@@ -27,17 +27,20 @@ def tile_picked_pair_lin_mul_sub_p_kernel(tc, x_words, x_scales, w, offs, out):
     nc = tc.nc
     with ExitStack() as ctx:
         keep = ctx.enter_context(tc.tile_pool(name="keep", bufs=1))
+        shared = ctx.enter_context(tc.tile_pool(name="shared", bufs=1))
         psum = ctx.enter_context(tc.psum_pool(name="psum", bufs=1))
 
         offsets = keep.tile([P, S // 16], U16, name="offsets")
-        byte_table = keep.tile([P, T], U8, name="byte_table", align_bytes=64)
+        byte_table = shared.tile([P, T], U8, name="byte_table", offset=3072)
         byte_picked = keep.tile([P, S], U8, name="byte_picked", align_bytes=64)
         x_plane = keep.tile([P, S], U8, name="x_plane", align_bytes=64)
-        word_table = [keep.tile([P, T], U32, name="word_table%d" % o, align_bytes=64) for o in range(PASSES)]
+        word_table = [shared.tile([P, T], U32, name="word_table0", offset=8192),
+                      keep.tile([P, T], U32, name="word_table1", align_bytes=64)]
         w_raw = {}
-        for d in range(D):
-            for o in range(PASSES):
-                w_raw[d, o] = keep.tile([P, PACK, N], F32, name="w_raw%d%d" % (d, o), align_bytes=64)
+        w_raw[0, 0] = keep.tile([P, PACK, N], F32, name="w_raw00", tag="x_codes1", align_bytes=64)
+        w_raw[0, 1] = shared.tile([P, PACK, N], F32, name="w_raw01", offset=0)
+        w_raw[1, 0] = shared.tile([P, PACK, N], F32, name="w_raw10", offset=4096)
+        w_raw[1, 1] = shared.tile([P, PACK, N], F32, name="w_raw11", offset=8192)
 
         def load_words(o):
             nc.sync.dma_start(out=word_table[o][:].bitcast(I32),
@@ -56,36 +59,36 @@ def tile_picked_pair_lin_mul_sub_p_kernel(tc, x_words, x_scales, w, offs, out):
         load_words(0)
         load_w(0, 0)
         load_words(1)
-        load_w(0, 1)
-        load_w(1, 0)
-        load_w(1, 1)
 
         nc.vector.tensor_copy(byte_picked[:], byte_table[:].indirect(offsets[:]))
         for q in range(4):
-            nc.scalar.dma_start(out=x_plane[QUAD * q:QUAD * q + 8, :].bitcast(I32),
-                                in_=byte_picked[ROWS0 + q:P:4, :].bitcast(I32))
+            nc.sync.dma_start(out=x_plane[QUAD * q:QUAD * q + 8, :].bitcast(I32),
+                              in_=byte_picked[ROWS0 + q:P:4, :].bitcast(I32))
+        load_w(0, 1)
+        load_w(1, 0)
 
         x_codes = {}
 
-        def gather_words(d, o):
-            x_codes[d, o] = keep.tile([P, V], U32, name="x_codes%d%d" % (d, o), align_bytes=64)
-            cols = slice(d * V // 16, (d + 1) * V // 16)
-            nc.vector.tensor_copy(x_codes[d, o][:], word_table[o][:].indirect(offsets[:, cols]))
+        def gather_words(o, a, b):
+            x_codes[o] = keep.tile([P, S], U32, name="x_codes%d" % o, tag="x_codes%d" % o, align_bytes=64)
+            nc.vector.tensor_copy(x_codes[o][:, a:b], word_table[o][:].indirect(offsets[:, a // 16:b // 16]))
 
         w_bf = {}
         w_codes = {}
         w_scales = {}
 
-        def cast_w(d, o, mt, copy):
-            w_bf[d, o, mt] = keep.tile([P, P * PACK], BF16, name="w_bf%d%d%d" % (d, o, mt), align_bytes=64)
-            copy(w_bf[d, o, mt][:].rearrange("p (c i j) -> p c j i", i=4, j=PACK),
-                 w_raw[d, o][:, :, mt * P:(mt + 1) * P].rearrange("p j (c i) -> p c j i", i=4))
+        def cast_w(d, o, a, b, copy):
+            w_bf[d, o, a] = keep.tile([P, (b - a) * PACK], BF16, name="w_bf%d%d_%d" % (d, o, a), align_bytes=64)
+            copy(w_bf[d, o, a][:].rearrange("p (c i j) -> p c j i", i=2, j=PACK),
+                 w_raw[d, o][:, :, a:b].rearrange("p j (c i) -> p c j i", i=2))
 
-        def quantize_w(d, o, mt):
-            w_codes[d, o, mt] = keep.tile([P, P], U32, name="w_codes%d%d%d" % (d, o, mt), align_bytes=64)
-            w_scales[d, o, mt] = keep.tile([P, P], U8, name="w_scales%d%d%d" % (d, o, mt), align_bytes=64)
-            nc.vector.quantize_mx(out=w_codes[d, o, mt][:].bitcast(FP8X4), scales=w_scales[d, o, mt][:],
-                                  in_=w_bf[d, o, mt][:])
+        def quantize_w(d, o, a, b):
+            codes = keep.tile([P, b - a], U32, name="w_codes%d%d_%d" % (d, o, a), align_bytes=64)
+            scales = keep.tile([P, b - a], U8, name="w_scales%d%d_%d" % (d, o, a), align_bytes=64)
+            nc.vector.quantize_mx(out=codes[:].bitcast(FP8X4), scales=scales[:], in_=w_bf[d, o, a][:])
+            for m in range(a, b, P):
+                w_codes[d, o, m // P] = codes[:, m - a:m - a + P]
+                w_scales[d, o, m // P] = scales[:, m - a:m - a + P]
 
         acc = {}
         for d in range(D):
@@ -95,43 +98,57 @@ def tile_picked_pair_lin_mul_sub_p_kernel(tc, x_words, x_scales, w, offs, out):
 
         def multiply(d, o, mt):
             for a, b in CHUNKS:
+                cols = slice(d * V + a, d * V + b)
                 nc.tensor.matmul_mx(out=acc[d, mt, a][:],
-                                    lhsT=w_codes[d, o, mt][:].bitcast(FP8X4), lhsT_scale=w_scales[d, o, mt][:],
-                                    rhs=x_codes[d, o][:, a:b].bitcast(FP8X4),
-                                    rhs_scale=x_plane[4 * o:P, d * V + a:d * V + b],
+                                    lhsT=w_codes[d, o, mt].bitcast(FP8X4), lhsT_scale=w_scales[d, o, mt],
+                                    rhs=x_codes[o][:, cols].bitcast(FP8X4),
+                                    rhs_scale=x_plane[4 * o:P, cols],
                                     start=(o == 0), stop=(o == PASSES - 1))
 
-        gather_words(0, 0)
-        gather_words(1, 0)
+        gather_words(0, 0, S)
+        load_w(1, 1)
+        cast_w(0, 0, 0, N, nc.scalar.copy)
+        quantize_w(0, 0, 0, N)
+        gather_words(1, 0, S)
+        cast_w(0, 1, 0, N, nc.scalar.copy)
+        quantize_w(0, 1, 0, N)
         for mt in range(M_TILES):
-            cast_w(0, 0, mt, nc.scalar.copy)
-        for mt in range(M_TILES):
-            quantize_w(0, 0, mt)
             multiply(0, 0, mt)
-        gather_words(0, 1)
-        gather_words(1, 1)
         for mt in range(M_TILES):
-            cast_w(0, 1, mt, nc.scalar.copy)
+            nc.tensor.matmul_mx(out=acc[1, mt, 0][:],
+                                lhsT=w_codes[0, 0, mt].bitcast(FP8X4), lhsT_scale=w_scales[0, 0, mt],
+                                rhs=x_codes[0][:, 0:512].bitcast(FP8X4), rhs_scale=x_plane[:, 0:512],
+                                start=True, stop=True)
         for mt in range(M_TILES):
-            quantize_w(0, 1, mt)
             multiply(0, 1, mt)
-        for mt in range(M_TILES):
-            cast_w(1, 0, mt, nc.scalar.copy)
-        for mt in range(M_TILES):
-            cast_w(1, 1, mt, nc.vector.tensor_copy)
-        for mt in range(M_TILES):
-            for o in range(PASSES):
-                quantize_w(1, o, mt)
+        cast_w(1, 0, 0, P, nc.scalar.copy)
+        cast_w(1, 0, P, N, nc.scalar.copy)
+        cast_w(1, 1, 0, P, nc.vector.tensor_copy)
+        cast_w(1, 1, P, N, nc.scalar.copy)
+        for o in range(PASSES):
+            for mt in range(M_TILES):
+                quantize_w(1, o, mt * P, (mt + 1) * P)
                 multiply(1, o, mt)
 
-        y0 = {}
+        y0 = [shared.tile([P, V], F32, name="y0_%d" % mt, offset=8192 + 4 * V * mt) for mt in range(M_TILES)]
+        res = [keep.tile([P, V], F32, name="res%d" % mt, align_bytes=64) for mt in range(M_TILES)]
         for mt in range(M_TILES):
             for a, b in CHUNKS:
-                y0[mt, a] = keep.tile([P, b - a], F32, name="y0_%d_%d" % (mt, a), align_bytes=64)
-                nc.scalar.copy(y0[mt, a][:], acc[0, mt, a][:])
-        for mt in range(M_TILES):
-            for a, b in CHUNKS:
-                res = keep.tile([P, b - a], F32, name="res%d_%d" % (mt, a), align_bytes=64)
-                nc.vector.tensor_tensor(res[:], acc[1, mt, a][:], y0[mt, a][:], mybir.AluOpType.mult)
-                queue = nc.sync if a == 0 else nc.scalar
-                queue.dma_start(out=out[mt * P:(mt + 1) * P, a:b], in_=res[:])
+                nc.scalar.copy(y0[mt][:, a:b], acc[0, mt, a][:])
+
+        def product(mt, bank, a, b):
+            nc.vector.tensor_tensor(res[mt][:, a:b], acc[1, mt, bank][:, a - bank:b - bank], y0[mt][:, a:b],
+                                    mybir.AluOpType.mult)
+
+        def store(queue, mt, a, b):
+            queue.dma_start(out=out[mt * P:(mt + 1) * P, a:b], in_=res[mt][:, a:b])
+
+        product(0, 0, 0, 512)
+        product(0, 512, 512, V)
+        store(nc.sync, 0, 0, V)
+        product(1, 0, 0, 256)
+        store(nc.scalar, 1, 0, 256)
+        product(1, 0, 256, 512)
+        store(nc.sync, 1, 256, 512)
+        product(1, 512, 512, V)
+        store(nc.scalar, 1, 512, V)

@@ -40,7 +40,7 @@ def tile_picked_pair_lin_mul_sub_p_kernel(tc, x_words, x_scales, w, offs, out):
         w_raw[0, 0] = keep.tile([P, PACK, N], F32, name="w_raw00", tag="x_codes1", align_bytes=64)
         w_raw[0, 1] = shared.tile([P, PACK, N], F32, name="w_raw01", offset=0)
         w_raw[1, 0] = shared.tile([P, PACK, N], F32, name="w_raw10", offset=4096)
-        w_raw[1, 1] = shared.tile([P, PACK, N], F32, name="w_raw11", offset=8192)
+        w_last = [shared.tile([P, PACK, P], F32, name="w_last%d" % mt, offset=8192 + 2048 * mt) for mt in range(M_TILES)]
 
         def load_words(o):
             nc.sync.dma_start(out=word_table[o][:].bitcast(I32),
@@ -79,11 +79,13 @@ def tile_picked_pair_lin_mul_sub_p_kernel(tc, x_words, x_scales, w, offs, out):
 
         def cast_w(d, o, a, b, copy):
             w_bf[d, o, a] = keep.tile([P, (b - a) * PACK], BF16, name="w_bf%d%d_%d" % (d, o, a), align_bytes=64)
+            raw = w_last[a // P][:] if (d, o) == (1, 1) else w_raw[d, o][:, :, a:b]
             copy(w_bf[d, o, a][:].rearrange("p (c i j) -> p c j i", i=2, j=PACK),
-                 w_raw[d, o][:, :, a:b].rearrange("p j (c i) -> p c j i", i=2))
+                 raw.rearrange("p j (c i) -> p c j i", i=2))
 
         def quantize_w(d, o, a, b):
-            codes = keep.tile([P, b - a], U32, name="w_codes%d%d_%d" % (d, o, a), align_bytes=64)
+            codes = keep.tile([P, b - a], U32, name="w_codes%d%d_%d" % (d, o, a), align_bytes=64,
+                              tag="w_bf11_0" if (d, o, a) == (1, 0, P) else "w_codes%d%d_%d" % (d, o, a))
             scales = keep.tile([P, b - a], U8, name="w_scales%d%d_%d" % (d, o, a), align_bytes=64)
             nc.vector.quantize_mx(out=codes[:].bitcast(FP8X4), scales=scales[:], in_=w_bf[d, o, a][:])
             for m in range(a, b, P):
@@ -106,7 +108,9 @@ def tile_picked_pair_lin_mul_sub_p_kernel(tc, x_words, x_scales, w, offs, out):
                                     start=(o == 0), stop=(o == PASSES - 1))
 
         gather_words(0, 0, S)
-        load_w(1, 1)
+        for mt in range(M_TILES):
+            nc.sync.dma_start(out=w_last[mt][:],
+                              in_=w[1, K_PASS:, mt * P:(mt + 1) * P].rearrange("(p j) m -> p j m", j=PACK))
         cast_w(0, 0, 0, N, nc.scalar.copy)
         quantize_w(0, 0, 0, N)
         gather_words(1, 0, S)
@@ -121,23 +125,25 @@ def tile_picked_pair_lin_mul_sub_p_kernel(tc, x_words, x_scales, w, offs, out):
                                 start=True, stop=True)
         for mt in range(M_TILES):
             multiply(0, 1, mt)
-        cast_w(1, 0, 0, P, nc.scalar.copy)
-        cast_w(1, 0, P, N, nc.scalar.copy)
-        cast_w(1, 1, 0, P, nc.vector.tensor_copy)
-        cast_w(1, 1, P, N, nc.scalar.copy)
         for o in range(PASSES):
-            for mt in range(M_TILES):
+            cast_w(1, o, 0, P, nc.vector.tensor_copy)
+            cast_w(1, o, P, N, nc.scalar.copy)
+        for mt in range(M_TILES):
+            for o in range(PASSES):
                 quantize_w(1, o, mt * P, (mt + 1) * P)
                 multiply(1, o, mt)
 
-        y0 = [shared.tile([P, V], F32, name="y0_%d" % mt, offset=8192 + 4 * V * mt) for mt in range(M_TILES)]
+        y0 = {(0, 0): shared.tile([P, 512], F32, name="y0_00", offset=8704),
+              (0, 512): shared.tile([P, 128], F32, name="y0_01", offset=10752),
+              (1, 0): shared.tile([P, 512], F32, name="y0_10", offset=11776),
+              (1, 512): shared.tile([P, 128], F32, name="y0_11", offset=11264)}
         res = [keep.tile([P, V], F32, name="res%d" % mt, align_bytes=64) for mt in range(M_TILES)]
         for mt in range(M_TILES):
             for a, b in CHUNKS:
-                nc.scalar.copy(y0[mt][:, a:b], acc[0, mt, a][:])
+                nc.scalar.copy(y0[mt, a][:], acc[0, mt, a][:])
 
         def product(mt, bank, a, b):
-            nc.vector.tensor_tensor(res[mt][:, a:b], acc[1, mt, bank][:, a - bank:b - bank], y0[mt][:, a:b],
+            nc.vector.tensor_tensor(res[mt][:, a:b], acc[1, mt, bank][:, a - bank:b - bank], y0[mt, bank][:, a - bank:b - bank],
                                     mybir.AluOpType.mult)
 
         def store(queue, mt, a, b):

@@ -20,7 +20,7 @@ PASSES = K // K_PASS
 M_TILES = N // P
 QUAD = 32
 ROWS0 = 96
-CHUNKS = ((0, 512), (512, 640))
+BANKS = ((0, 512), (512, 640))
 
 
 def tile_picked_pair_lin_mul_sub_p_kernel(tc, x_words, x_scales, w, offs, out):
@@ -34,21 +34,21 @@ def tile_picked_pair_lin_mul_sub_p_kernel(tc, x_words, x_scales, w, offs, out):
         byte_table = shared.tile([P, T], U8, name="byte_table", offset=3072)
         byte_picked = keep.tile([P, S], U8, name="byte_picked", align_bytes=64)
         x_plane = keep.tile([P, S], U8, name="x_plane", align_bytes=64)
-        word_table = [shared.tile([P, T], U32, name="word_table0", offset=8192),
-                      keep.tile([P, T], U32, name="word_table1", align_bytes=64)]
+        word_table = [keep.tile([P, T], U32, name="word_table%d" % o, align_bytes=64) for o in range(PASSES)]
         w_raw = {}
-        w_raw[0, 0] = keep.tile([P, PACK, N], F32, name="w_raw00", tag="x_codes1", align_bytes=64)
-        w_raw[0, 1] = shared.tile([P, PACK, N], F32, name="w_raw01", offset=0)
-        w_raw[1, 0] = shared.tile([P, PACK, N], F32, name="w_raw10", offset=4096)
-        w_last = [shared.tile([P, PACK, P], F32, name="w_last%d" % mt, offset=8192 + 2048 * mt) for mt in range(M_TILES)]
+        w_raw[0, 0, 0] = shared.tile([P, PACK, N], F32, name="w_raw00", offset=8192)
+        w_raw[0, 1, 0] = keep.tile([P, PACK, N], F32, name="w_raw01", align_bytes=64)
+        w_raw[1, 0, 0] = shared.tile([P, PACK, N], F32, name="w_raw10", offset=0)
+        w_raw[1, 1, 0] = shared.tile([P, PACK, P], F32, name="w_raw11a", offset=4096)
+        w_raw[1, 1, P] = shared.tile([P, PACK, P], F32, name="w_raw11b", offset=8192)
 
         def load_words(o):
             nc.sync.dma_start(out=word_table[o][:].bitcast(I32),
                               in_=x_words[o].rearrange("p n t -> p (n t)").bitcast(I32))
 
-        def load_w(d, o):
-            nc.sync.dma_start(out=w_raw[d, o][:],
-                              in_=w[d, o * K_PASS:(o + 1) * K_PASS, :].rearrange("(p j) m -> p j m", j=PACK))
+        def load_w(d, o, a, b):
+            nc.sync.dma_start(out=w_raw[d, o, a][:],
+                              in_=w[d, o * K_PASS:(o + 1) * K_PASS, a:b].rearrange("(p j) m -> p j m", j=PACK))
 
         nc.vector.memset(byte_table[0:ROWS0, :].bitcast(I32), 0)
         nc.gpsimd.memset(x_plane[:].bitcast(I32), 0)
@@ -57,35 +57,37 @@ def tile_picked_pair_lin_mul_sub_p_kernel(tc, x_words, x_scales, w, offs, out):
             nc.sync.dma_start(out=byte_table[ROWS0 + 16 * o:ROWS0 + 16 * (o + 1), :].bitcast(I32),
                               in_=x_scales[o].rearrange("(q j) c -> j q c", j=4).bitcast(I32))
         load_words(0)
-        load_w(0, 0)
+        load_w(0, 0, 0, N)
         load_words(1)
+        load_w(0, 1, 0, N)
 
         nc.vector.tensor_copy(byte_picked[:], byte_table[:].indirect(offsets[:]))
         for q in range(4):
             nc.sync.dma_start(out=x_plane[QUAD * q:QUAD * q + 8, :].bitcast(I32),
                               in_=byte_picked[ROWS0 + q:P:4, :].bitcast(I32))
-        load_w(0, 1)
-        load_w(1, 0)
+        load_w(1, 0, 0, N)
+        load_w(1, 1, 0, P)
+        load_w(1, 1, P, N)
 
         x_codes = {}
 
-        def gather_words(o, a, b):
-            x_codes[o] = keep.tile([P, S], U32, name="x_codes%d" % o, tag="x_codes%d" % o, align_bytes=64)
-            nc.vector.tensor_copy(x_codes[o][:, a:b], word_table[o][:].indirect(offsets[:, a // 16:b // 16]))
+        def gather_words(o, offset):
+            x_codes[o] = shared.tile([P, S], U32, name="x_codes%d" % o, offset=offset, align_bytes=64)
+            nc.vector.tensor_copy(x_codes[o][:], word_table[o][:].indirect(offsets[:]))
 
         w_bf = {}
         w_codes = {}
         w_scales = {}
 
-        def cast_w(d, o, a, b, copy):
-            w_bf[d, o, a] = keep.tile([P, (b - a) * PACK], BF16, name="w_bf%d%d_%d" % (d, o, a), align_bytes=64)
-            raw = w_last[a // P][:] if (d, o) == (1, 1) else w_raw[d, o][:, :, a:b]
+        def cast_w(d, o, a, b, offset, copy):
+            name = "w_bf%d%d_%d" % (d, o, a)
+            w_bf[d, o, a] = shared.tile([P, (b - a) * PACK], BF16, name=name, offset=offset, align_bytes=64)
+            raw = w_raw[d, o, a][:, :, 0:b - a] if (d, o, a) in w_raw else w_raw[d, o, 0][:, :, a:b]
             copy(w_bf[d, o, a][:].rearrange("p (c i j) -> p c j i", i=2, j=PACK),
                  raw.rearrange("p j (c i) -> p c j i", i=2))
 
         def quantize_w(d, o, a, b):
-            codes = keep.tile([P, b - a], U32, name="w_codes%d%d_%d" % (d, o, a), align_bytes=64,
-                              tag="w_bf11_0" if (d, o, a) == (1, 0, P) else "w_codes%d%d_%d" % (d, o, a))
+            codes = keep.tile([P, b - a], U32, name="w_codes%d%d_%d" % (d, o, a), align_bytes=64)
             scales = keep.tile([P, b - a], U8, name="w_scales%d%d_%d" % (d, o, a), align_bytes=64)
             nc.vector.quantize_mx(out=codes[:].bitcast(FP8X4), scales=scales[:], in_=w_bf[d, o, a][:])
             for m in range(a, b, P):
@@ -95,11 +97,11 @@ def tile_picked_pair_lin_mul_sub_p_kernel(tc, x_words, x_scales, w, offs, out):
         acc = {}
         for d in range(D):
             for mt in range(M_TILES):
-                for a, b in CHUNKS:
+                for a, b in BANKS:
                     acc[d, mt, a] = psum.tile([P, b - a], F32, name="acc%d%d_%d" % (d, mt, a))
 
         def multiply(d, o, mt):
-            for a, b in CHUNKS:
+            for a, b in BANKS:
                 cols = slice(d * V + a, d * V + b)
                 nc.tensor.matmul_mx(out=acc[d, mt, a][:],
                                     lhsT=w_codes[d, o, mt].bitcast(FP8X4), lhsT_scale=w_scales[d, o, mt],
@@ -107,43 +109,41 @@ def tile_picked_pair_lin_mul_sub_p_kernel(tc, x_words, x_scales, w, offs, out):
                                     rhs_scale=x_plane[4 * o:P, cols],
                                     start=(o == 0), stop=(o == PASSES - 1))
 
-        gather_words(0, 0, S)
-        for mt in range(M_TILES):
-            nc.sync.dma_start(out=w_last[mt][:],
-                              in_=w[1, K_PASS:, mt * P:(mt + 1) * P].rearrange("(p j) m -> p j m", j=PACK))
-        cast_w(0, 0, 0, N, nc.scalar.copy)
+        gather_words(0, 12288)
+        cast_w(0, 0, 0, N, 17408, nc.scalar.copy)
         quantize_w(0, 0, 0, N)
-        gather_words(1, 0, S)
-        cast_w(0, 1, 0, N, nc.scalar.copy)
+        gather_words(1, 17408)
+        cast_w(0, 1, 0, N, 22528, nc.scalar.copy)
         quantize_w(0, 1, 0, N)
         for mt in range(M_TILES):
             multiply(0, 0, mt)
-        for mt in range(M_TILES):
-            nc.tensor.matmul_mx(out=acc[1, mt, 0][:],
-                                lhsT=w_codes[0, 0, mt].bitcast(FP8X4), lhsT_scale=w_scales[0, 0, mt],
-                                rhs=x_codes[0][:, 0:512].bitcast(FP8X4), rhs_scale=x_plane[:, 0:512],
-                                start=True, stop=True)
+        nc.tensor.matmul_mx(out=acc[1, 1, 0][:],
+                            lhsT=w_codes[0, 0, 1].bitcast(FP8X4), lhsT_scale=w_scales[0, 0, 1],
+                            rhs=x_codes[0][:, 0:512].bitcast(FP8X4), rhs_scale=x_plane[:, 0:512],
+                            start=True, stop=True)
         for mt in range(M_TILES):
             multiply(0, 1, mt)
-        for o in range(PASSES):
-            cast_w(1, o, 0, P, nc.vector.tensor_copy)
-            cast_w(1, o, P, N, nc.scalar.copy)
+        cast_w(1, 0, 0, P, 24576, nc.scalar.copy)
+        cast_w(1, 0, P, N, 25600, nc.scalar.copy)
+        cast_w(1, 1, 0, P, 26624, nc.vector.tensor_copy)
+        quantize_w(1, 0, 0, P)
+        quantize_w(1, 1, 0, P)
+        cast_w(1, 1, P, N, 29184, nc.vector.tensor_copy)
+        quantize_w(1, 0, P, N)
+        quantize_w(1, 1, P, N)
         for mt in range(M_TILES):
             for o in range(PASSES):
-                quantize_w(1, o, mt * P, (mt + 1) * P)
                 multiply(1, o, mt)
 
-        y0 = {(0, 0): shared.tile([P, 512], F32, name="y0_00", offset=8704),
-              (0, 512): shared.tile([P, 128], F32, name="y0_01", offset=10752),
-              (1, 0): shared.tile([P, 512], F32, name="y0_10", offset=11776),
-              (1, 512): shared.tile([P, 128], F32, name="y0_11", offset=11264)}
-        res = [keep.tile([P, V], F32, name="res%d" % mt, align_bytes=64) for mt in range(M_TILES)]
+        y0 = [shared.tile([P, V], F32, name="y0_%d" % mt, offset=512 + 2560 * mt) for mt in range(M_TILES)]
+        res = [shared.tile([P, V], F32, name="res0", offset=27648, align_bytes=64),
+               keep.tile([P, V], F32, name="res1", align_bytes=64)]
         for mt in range(M_TILES):
-            for a, b in CHUNKS:
-                nc.scalar.copy(y0[mt, a][:], acc[0, mt, a][:])
+            for a, b in BANKS:
+                nc.scalar.copy(y0[mt][:, a:b], acc[0, mt, a][:])
 
         def product(mt, bank, a, b):
-            nc.vector.tensor_tensor(res[mt][:, a:b], acc[1, mt, bank][:, a - bank:b - bank], y0[mt, bank][:, a - bank:b - bank],
+            nc.vector.tensor_tensor(res[mt][:, a:b], acc[1, mt, bank][:, a - bank:b - bank], y0[mt][:, a:b],
                                     mybir.AluOpType.mult)
 
         def store(queue, mt, a, b):

@@ -20,7 +20,8 @@ PASSES = K // K_PASS
 M_TILES = N // P
 QUAD = 32
 ROWS0 = 96
-BANKS = ((0, 512), (512, 640))
+BANKS = ((0, 256), (256, 640))
+PIECE = 256
 
 
 def tile_picked_pair_lin_mul_sub_p_kernel(tc, x_words, x_scales, w, offs, out):
@@ -37,10 +38,10 @@ def tile_picked_pair_lin_mul_sub_p_kernel(tc, x_words, x_scales, w, offs, out):
         word_table = [keep.tile([P, T], U32, name="word_table%d" % o, align_bytes=64) for o in range(PASSES)]
         w_raw = {}
         w_raw[0, 0, 0] = shared.tile([P, PACK, N], F32, name="w_raw00", offset=8192)
-        w_raw[0, 1, 0] = keep.tile([P, PACK, N], F32, name="w_raw01", align_bytes=64)
-        w_raw[1, 0, 0] = shared.tile([P, PACK, N], F32, name="w_raw10", offset=0)
-        w_raw[1, 1, 0] = shared.tile([P, PACK, P], F32, name="w_raw11a", offset=4096)
-        w_raw[1, 1, P] = shared.tile([P, PACK, P], F32, name="w_raw11b", offset=8192)
+        w_raw[0, 1, 0] = shared.tile([P, PACK, N], F32, name="w_raw01", offset=0)
+        w_raw[1, 0, 0] = shared.tile([P, PACK, N], F32, name="w_raw10", offset=4096)
+        w_raw[1, 1, 0] = shared.tile([P, PACK, P], F32, name="w_raw11a", offset=8192)
+        w_raw[1, 1, P] = shared.tile([P, PACK, P], F32, name="w_raw11b", offset=10240)
 
         def load_words(o):
             nc.sync.dma_start(out=word_table[o][:].bitcast(I32),
@@ -59,12 +60,12 @@ def tile_picked_pair_lin_mul_sub_p_kernel(tc, x_words, x_scales, w, offs, out):
         load_words(0)
         load_w(0, 0, 0, N)
         load_words(1)
-        load_w(0, 1, 0, N)
 
         nc.vector.tensor_copy(byte_picked[:], byte_table[:].indirect(offsets[:]))
         for q in range(4):
             nc.sync.dma_start(out=x_plane[QUAD * q:QUAD * q + 8, :].bitcast(I32),
                               in_=byte_picked[ROWS0 + q:P:4, :].bitcast(I32))
+        load_w(0, 1, 0, N)
         load_w(1, 0, 0, N)
         load_w(1, 1, 0, P)
         load_w(1, 1, P, N)
@@ -98,29 +99,33 @@ def tile_picked_pair_lin_mul_sub_p_kernel(tc, x_words, x_scales, w, offs, out):
         for d in range(D):
             for mt in range(M_TILES):
                 for a, b in BANKS:
-                    acc[d, mt, a] = psum.tile([P, b - a], F32, name="acc%d%d_%d" % (d, mt, a))
+                    acc[d, mt, a] = psum.tile([P, 512], F32, name="acc%d%d_%d" % (d, mt, a))
 
         def multiply(d, o, mt):
             for a, b in BANKS:
-                cols = slice(d * V + a, d * V + b)
-                nc.tensor.matmul_mx(out=acc[d, mt, a][:],
-                                    lhsT=w_codes[d, o, mt].bitcast(FP8X4), lhsT_scale=w_scales[d, o, mt],
-                                    rhs=x_codes[o][:, cols].bitcast(FP8X4),
-                                    rhs_scale=x_plane[4 * o:P, cols],
-                                    start=(o == 0), stop=(o == PASSES - 1))
+                for lo in range(a, b, PIECE):
+                    hi = min(lo + PIECE, b)
+                    cols = slice(d * V + lo, d * V + hi)
+                    nc.tensor.matmul_mx(out=acc[d, mt, a][:, lo - a:hi - a],
+                                        lhsT=w_codes[d, o, mt].bitcast(FP8X4), lhsT_scale=w_scales[d, o, mt],
+                                        rhs=x_codes[o][:, cols].bitcast(FP8X4),
+                                        rhs_scale=x_plane[4 * o:P, cols],
+                                        start=(o == 0 and lo == a), stop=(o == PASSES - 1 and hi == b))
 
         gather_words(0, 12288)
         cast_w(0, 0, 0, N, 17408, nc.scalar.copy)
         quantize_w(0, 0, 0, N)
         gather_words(1, 17408)
-        cast_w(0, 1, 0, N, 22528, nc.scalar.copy)
-        quantize_w(0, 1, 0, N)
+        for mt in range(M_TILES):
+            cast_w(0, 1, mt * P, (mt + 1) * P, 22528 + 1024 * mt, nc.scalar.copy)
+            quantize_w(0, 1, mt * P, (mt + 1) * P)
         for mt in range(M_TILES):
             multiply(0, 0, mt)
-        nc.tensor.matmul_mx(out=acc[1, 1, 0][:],
-                            lhsT=w_codes[0, 0, 1].bitcast(FP8X4), lhsT_scale=w_scales[0, 0, 1],
-                            rhs=x_codes[0][:, 0:512].bitcast(FP8X4), rhs_scale=x_plane[:, 0:512],
-                            start=True, stop=True)
+        for mt in range(M_TILES):
+            nc.tensor.matmul_mx(out=acc[1, mt, 0][:],
+                                lhsT=w_codes[0, 0, mt].bitcast(FP8X4), lhsT_scale=w_scales[0, 0, mt],
+                                rhs=x_codes[0][:, 0:512].bitcast(FP8X4), rhs_scale=x_plane[:, 0:512],
+                                start=True, stop=True)
         for mt in range(M_TILES):
             multiply(0, 1, mt)
         cast_w(1, 0, 0, P, 24576, nc.scalar.copy)
@@ -135,12 +140,12 @@ def tile_picked_pair_lin_mul_sub_p_kernel(tc, x_words, x_scales, w, offs, out):
             for o in range(PASSES):
                 multiply(1, o, mt)
 
-        y0 = [shared.tile([P, V], F32, name="y0_%d" % mt, offset=512 + 2560 * mt) for mt in range(M_TILES)]
-        res = [shared.tile([P, V], F32, name="res0", offset=27648, align_bytes=64),
+        y0 = [shared.tile([P, V], F32, name="y0_%d" % mt, offset=4608 + 2560 * mt) for mt in range(M_TILES)]
+        res = [shared.tile([P, V], F32, name="res0", offset=28672, align_bytes=64),
                keep.tile([P, V], F32, name="res1", align_bytes=64)]
         for mt in range(M_TILES):
             for a, b in BANKS:
-                nc.scalar.copy(y0[mt][:, a:b], acc[0, mt, a][:])
+                nc.scalar.copy(y0[mt][:, a:b], acc[0, mt, a][:, 0:b - a])
 
         def product(mt, bank, a, b):
             nc.vector.tensor_tensor(res[mt][:, a:b], acc[1, mt, bank][:, a - bank:b - bank], y0[mt][:, a:b],
@@ -149,12 +154,12 @@ def tile_picked_pair_lin_mul_sub_p_kernel(tc, x_words, x_scales, w, offs, out):
         def store(queue, mt, a, b):
             queue.dma_start(out=out[mt * P:(mt + 1) * P, a:b], in_=res[mt][:, a:b])
 
-        product(0, 0, 0, 512)
-        product(0, 512, 512, V)
+        product(0, 0, 0, 256)
+        product(0, 256, 256, V)
         store(nc.sync, 0, 0, V)
         product(1, 0, 0, 256)
         store(nc.scalar, 1, 0, 256)
-        product(1, 0, 256, 512)
+        product(1, 256, 256, 512)
         store(nc.sync, 1, 256, 512)
-        product(1, 512, 512, V)
+        product(1, 256, 512, V)
         store(nc.scalar, 1, 512, V)

@@ -34,7 +34,7 @@ def tile_picked_pair_lin_mul_sub_p_kernel(tc, x_words, x_scales, w, offs, out):
         offsets = keep.tile([P, S // 16], U16, name="offsets")
         byte_table = shared.tile([P, T], U8, name="byte_table", offset=3072)
         byte_picked = keep.tile([P, S], U8, name="byte_picked", align_bytes=64)
-        x_plane = keep.tile([P, S], U8, name="x_plane", align_bytes=64)
+        x_plane = keep.tile([P, S + V], U8, name="x_plane", align_bytes=64)
         word_table = [keep.tile([P, T], U32, name="word_table%d" % o, align_bytes=64) for o in range(PASSES)]
         w_raw = {}
         w_raw[0, 0, 0] = shared.tile([P, PACK, N], F32, name="w_raw00", offset=8192)
@@ -54,19 +54,24 @@ def tile_picked_pair_lin_mul_sub_p_kernel(tc, x_words, x_scales, w, offs, out):
         nc.vector.memset(byte_table[0:ROWS0, :].bitcast(I32), 0)
         nc.gpsimd.memset(x_plane[:].bitcast(I32), 0)
         nc.sync.dma_start(offsets[:], offs)
-        for o in range(PASSES):
-            nc.sync.dma_start(out=byte_table[ROWS0 + 16 * o:ROWS0 + 16 * (o + 1), :].bitcast(I32),
-                              in_=x_scales[o].rearrange("(q j) c -> j q c", j=4).bitcast(I32))
+        nc.sync.dma_start(out=byte_table[ROWS0:P, :].bitcast(I32),
+                          in_=x_scales.rearrange("o r c -> (o r) c").bitcast(I32))
         load_words(0)
         load_w(0, 0, 0, N)
         load_words(1)
 
         nc.vector.tensor_copy(byte_picked[:], byte_table[:].indirect(offsets[:]))
-        for q in range(4):
-            nc.sync.dma_start(out=x_plane[QUAD * q:QUAD * q + 8, :].bitcast(I32),
-                              in_=byte_picked[ROWS0 + q:P:4, :].bitcast(I32))
+
+        def move_scales(o):
+            for q in range(4):
+                row = ROWS0 + 16 * o + 4 * q
+                nc.sync.dma_start(out=x_plane[QUAD * q + 4 * o:QUAD * q + 4 * o + 4, o * V:o * V + S].bitcast(I32),
+                                  in_=byte_picked[row:row + 4, :].bitcast(I32))
+
+        move_scales(0)
         load_w(0, 1, 0, N)
         load_w(1, 0, 0, N)
+        move_scales(1)
         load_w(1, 1, 0, P)
         load_w(1, 1, P, N)
 
@@ -88,7 +93,10 @@ def tile_picked_pair_lin_mul_sub_p_kernel(tc, x_words, x_scales, w, offs, out):
                  raw.rearrange("p j (c i) -> p c j i", i=2))
 
         def quantize_w(d, o, a, b):
-            codes = keep.tile([P, b - a], U32, name="w_codes%d%d_%d" % (d, o, a), align_bytes=64)
+            if (d, o, a) == (1, 0, P):
+                codes = shared.tile([P, b - a], U32, name="w_codes10_128", offset=26624, align_bytes=64)
+            else:
+                codes = keep.tile([P, b - a], U32, name="w_codes%d%d_%d" % (d, o, a), align_bytes=64)
             scales = keep.tile([P, b - a], U8, name="w_scales%d%d_%d" % (d, o, a), align_bytes=64)
             nc.vector.quantize_mx(out=codes[:].bitcast(FP8X4), scales=scales[:], in_=w_bf[d, o, a][:])
             for m in range(a, b, P):
@@ -109,7 +117,7 @@ def tile_picked_pair_lin_mul_sub_p_kernel(tc, x_words, x_scales, w, offs, out):
                     nc.tensor.matmul_mx(out=acc[d, mt, a][:, lo - a:hi - a],
                                         lhsT=w_codes[d, o, mt].bitcast(FP8X4), lhsT_scale=w_scales[d, o, mt],
                                         rhs=x_codes[o][:, cols].bitcast(FP8X4),
-                                        rhs_scale=x_plane[4 * o:P, cols],
+                                        rhs_scale=x_plane[4 * o:P, (o + d) * V + lo:(o + d) * V + hi],
                                         start=(o == 0 and lo == a), stop=(o == PASSES - 1 and hi == b))
 
         gather_words(0, 12288)

@@ -163,8 +163,9 @@ def tile_picked_pair_lin_mul_sub_p_kernel(tc, x_words, x_scales, w, offs, out):
             queue.dma_start(out=out[mt * P:(mt + 1) * P, a:b], in_=res[mt][:, a:b])
 
         product(0, 0, 0, 256)
+        store(nc.sync, 0, 0, 256)
         product(0, 256, 256, V)
-        store(nc.sync, 0, 0, V)
+        store(nc.sync, 0, 256, V)
         product(1, 0, 0, 256)
         store(nc.scalar, 1, 0, 256)
         product(1, 256, 256, 512)

@@ -21,7 +21,9 @@ M_TILES = N // P
 QUAD = 32
 ROWS0 = 96
 BANKS = ((0, 256), (256, 640))
-PIECE = 256
+PIECES = {0: ((0, 256),), 256: ((256, 384), (384, 640))}
+WALK = 2
+CUT = 1024
 
 
 def tile_picked_pair_lin_mul_sub_p_kernel(tc, x_words, x_scales, w, offs, out):
@@ -36,20 +38,17 @@ def tile_picked_pair_lin_mul_sub_p_kernel(tc, x_words, x_scales, w, offs, out):
         byte_picked = keep.tile([P, S], U8, name="byte_picked", align_bytes=64)
         x_plane = keep.tile([P, S + V], U8, name="x_plane", align_bytes=64)
         word_table = [keep.tile([P, T], U32, name="word_table%d" % o, align_bytes=64) for o in range(PASSES)]
+        raw_at = {(0, 0): 12288, (0, 1): 0, (1, 0): 4096, (1, 1): 15360}
         w_raw = {}
-        w_raw[0, 0, 0] = shared.tile([P, PACK, N], F32, name="w_raw00", offset=8192)
-        w_raw[0, 1, 0] = shared.tile([P, PACK, N], F32, name="w_raw01", offset=0)
-        w_raw[1, 0, 0] = shared.tile([P, PACK, N], F32, name="w_raw10", offset=4096)
-        w_raw[1, 1, 0] = shared.tile([P, PACK, P], F32, name="w_raw11a", offset=8192)
-        w_raw[1, 1, P] = shared.tile([P, PACK, P], F32, name="w_raw11b", offset=10240)
 
         def load_words(o):
             nc.sync.dma_start(out=word_table[o][:].bitcast(I32),
                               in_=x_words[o].rearrange("p n t -> p (n t)").bitcast(I32))
 
-        def load_w(d, o, a, b):
-            nc.sync.dma_start(out=w_raw[d, o, a][:],
-                              in_=w[d, o * K_PASS:(o + 1) * K_PASS, a:b].rearrange("(p j) m -> p j m", j=PACK))
+        def load_w(d, o):
+            w_raw[d, o] = shared.tile([P, PACK, N], F32, name="w_raw%d%d" % (d, o), offset=raw_at[d, o])
+            nc.sync.dma_start(out=w_raw[d, o][:],
+                              in_=w[d, o * K_PASS:(o + 1) * K_PASS, :].rearrange("(p j) m -> p j m", j=PACK))
 
         nc.vector.memset(byte_table[0:ROWS0, :].bitcast(I32), 0)
         nc.gpsimd.memset(x_plane[:].bitcast(I32), 0)
@@ -57,7 +56,7 @@ def tile_picked_pair_lin_mul_sub_p_kernel(tc, x_words, x_scales, w, offs, out):
         nc.sync.dma_start(out=byte_table[ROWS0:P, :].bitcast(I32),
                           in_=x_scales.rearrange("o r c -> (o r) c").bitcast(I32))
         load_words(0)
-        load_w(0, 0, 0, N)
+        load_w(0, 0)
         load_words(1)
 
         nc.vector.tensor_copy(byte_picked[:], byte_table[:].indirect(offsets[:]))
@@ -69,39 +68,37 @@ def tile_picked_pair_lin_mul_sub_p_kernel(tc, x_words, x_scales, w, offs, out):
                                   in_=byte_picked[row:row + 4, :].bitcast(I32))
 
         move_scales(0)
-        load_w(0, 1, 0, N)
-        load_w(1, 0, 0, N)
+        load_w(0, 1)
+        load_w(1, 0)
         move_scales(1)
-        load_w(1, 1, 0, P)
-        load_w(1, 1, P, N)
+        load_w(1, 1)
 
         x_codes = {}
 
-        def gather_words(o, offset):
-            x_codes[o] = shared.tile([P, S], U32, name="x_codes%d" % o, offset=offset, align_bytes=64)
-            nc.vector.tensor_copy(x_codes[o][:], word_table[o][:].indirect(offsets[:]))
+        def gather_words(o, a, b, offset):
+            picked = shared.tile([P, b - a], U32, name="x_codes%d_%d" % (o, a), offset=offset, align_bytes=64)
+            nc.vector.tensor_copy(picked[:], word_table[o][:].indirect(offsets[:, a // 16:b // 16]))
+            for lo in range(a, b, P):
+                x_codes[o, lo] = picked[:, lo - a:]
 
         w_bf = {}
         w_codes = {}
         w_scales = {}
 
-        def cast_w(d, o, a, b, offset, copy):
-            name = "w_bf%d%d_%d" % (d, o, a)
-            w_bf[d, o, a] = shared.tile([P, (b - a) * PACK], BF16, name=name, offset=offset, align_bytes=64)
-            raw = w_raw[d, o, a][:, :, 0:b - a] if (d, o, a) in w_raw else w_raw[d, o, 0][:, :, a:b]
-            copy(w_bf[d, o, a][:].rearrange("p (c i j) -> p c j i", i=2, j=PACK),
-                 raw.rearrange("p j (c i) -> p c j i", i=2))
+        def cast_w(d, o, a, b, copy, offset):
+            w_bf[d, o, a] = shared.tile([P, (b - a) * PACK], BF16, name="w_bf%d%d_%d" % (d, o, a), offset=offset,
+                                        align_bytes=64)
+            copy(w_bf[d, o, a][:].rearrange("p (c i j) -> p c j i", i=WALK, j=PACK),
+                 w_raw[d, o][:, :, a:b].rearrange("p j (c i) -> p c j i", i=WALK))
 
-        def quantize_w(d, o, a, b):
-            if (d, o, a) == (1, 0, P):
-                codes = shared.tile([P, b - a], U32, name="w_codes10_128", offset=26624, align_bytes=64)
-            else:
-                codes = keep.tile([P, b - a], U32, name="w_codes%d%d_%d" % (d, o, a), align_bytes=64)
+        def quantize_w(d, o, a, b, offset):
+            codes = shared.tile([P, b - a], U32, name="w_codes%d%d_%d" % (d, o, a), offset=offset, align_bytes=64)
             scales = keep.tile([P, b - a], U8, name="w_scales%d%d_%d" % (d, o, a), align_bytes=64)
             nc.vector.quantize_mx(out=codes[:].bitcast(FP8X4), scales=scales[:], in_=w_bf[d, o, a][:])
             for m in range(a, b, P):
                 w_codes[d, o, m // P] = codes[:, m - a:m - a + P]
                 w_scales[d, o, m // P] = scales[:, m - a:m - a + P]
+            return codes, scales
 
         acc = {}
         for d in range(D):
@@ -111,64 +108,60 @@ def tile_picked_pair_lin_mul_sub_p_kernel(tc, x_words, x_scales, w, offs, out):
 
         def multiply(d, o, mt):
             for a, b in BANKS:
-                for lo in range(a, b, PIECE):
-                    hi = min(lo + PIECE, b)
-                    cols = slice(d * V + lo, d * V + hi)
+                for lo, hi in PIECES[a]:
                     nc.tensor.matmul_mx(out=acc[d, mt, a][:, lo - a:hi - a],
                                         lhsT=w_codes[d, o, mt].bitcast(FP8X4), lhsT_scale=w_scales[d, o, mt],
-                                        rhs=x_codes[o][:, cols].bitcast(FP8X4),
+                                        rhs=x_codes[o, d * V + lo][:, 0:hi - lo].bitcast(FP8X4),
                                         rhs_scale=x_plane[4 * o:P, (o + d) * V + lo:(o + d) * V + hi],
                                         start=(o == 0 and lo == a), stop=(o == PASSES - 1 and hi == b))
 
-        gather_words(0, 12288)
-        cast_w(0, 0, 0, N, 17408, nc.scalar.copy)
-        quantize_w(0, 0, 0, N)
-        gather_words(1, 17408)
+        y0 = {}
+        res = [keep.tile([P, V], F32, name="res%d" % mt, align_bytes=64) for mt in range(M_TILES)]
+
+        def copy_y0(mt, bank, offset):
+            a, b = BANKS[bank]
+            y0[mt, a] = shared.tile([P, b - a], F32, name="y0_%d_%d" % (mt, a), offset=offset, align_bytes=64)
+            nc.scalar.copy(y0[mt, a][:], acc[0, mt, a][:, 0:b - a])
+
+        def product(mt, bank, a, b, queue):
+            nc.vector.tensor_tensor(res[mt][:, a:b], acc[1, mt, bank][:, a - bank:b - bank],
+                                    y0[mt, bank][:, a - bank:b - bank], mybir.AluOpType.mult)
+            queue.dma_start(out=out[mt * P:(mt + 1) * P, a:b], in_=res[mt][:, a:b])
+
+        gather_words(0, 0, S, 20480)
+        cast_w(0, 0, 0, N, nc.scalar.copy, 25600)
+        first_codes, first_scales = quantize_w(0, 0, 0, N, 32768)
         for mt in range(M_TILES):
-            cast_w(0, 1, mt * P, (mt + 1) * P, 22528 + 1024 * mt, nc.scalar.copy)
-            quantize_w(0, 1, mt * P, (mt + 1) * P)
+            nc.tensor.matmul_mx(out=acc[1, mt, 0][:, 0:N],
+                                lhsT=w_codes[0, 0, mt].bitcast(FP8X4), lhsT_scale=w_scales[0, 0, mt],
+                                rhs=first_codes[:].bitcast(FP8X4), rhs_scale=first_scales[:],
+                                start=True, stop=True)
+        gather_words(1, 0, CUT, 9216)
+        cast_w(0, 1, 0, N, nc.scalar.copy, 27648)
+        quantize_w(0, 1, 0, N, 33792)
+        gather_words(1, CUT, S, 0)
         for mt in range(M_TILES):
             multiply(0, 0, mt)
         for mt in range(M_TILES):
-            nc.tensor.matmul_mx(out=acc[1, mt, 0][:],
-                                lhsT=w_codes[0, 0, mt].bitcast(FP8X4), lhsT_scale=w_scales[0, 0, mt],
-                                rhs=x_codes[0][:, 0:512].bitcast(FP8X4), rhs_scale=x_plane[:, 0:512],
-                                start=True, stop=True)
-        for mt in range(M_TILES):
             multiply(0, 1, mt)
-        cast_w(1, 0, 0, P, 24576, nc.scalar.copy)
-        cast_w(1, 0, P, N, 25600, nc.scalar.copy)
-        cast_w(1, 1, 0, P, 26624, nc.vector.tensor_copy)
-        quantize_w(1, 0, 0, P)
-        quantize_w(1, 1, 0, P)
-        cast_w(1, 1, P, N, 29184, nc.vector.tensor_copy)
-        quantize_w(1, 0, P, N)
-        quantize_w(1, 1, P, N)
-        for mt in range(M_TILES):
-            for o in range(PASSES):
-                multiply(1, o, mt)
-
-        y0 = [shared.tile([P, V], F32, name="y0_%d" % mt, offset=4608 + 2560 * mt) for mt in range(M_TILES)]
-        res = [shared.tile([P, V], F32, name="res0", offset=28672, align_bytes=64),
-               keep.tile([P, V], F32, name="res1", align_bytes=64)]
-        for mt in range(M_TILES):
-            for a, b in BANKS:
-                nc.scalar.copy(y0[mt][:, a:b], acc[0, mt, a][:, 0:b - a])
-
-        def product(mt, bank, a, b):
-            nc.vector.tensor_tensor(res[mt][:, a:b], acc[1, mt, bank][:, a - bank:b - bank], y0[mt][:, a:b],
-                                    mybir.AluOpType.mult)
-
-        def store(queue, mt, a, b):
-            queue.dma_start(out=out[mt * P:(mt + 1) * P, a:b], in_=res[mt][:, a:b])
-
-        product(0, 0, 0, 256)
-        store(nc.sync, 0, 0, 256)
-        product(0, 256, 256, V)
-        store(nc.sync, 0, 256, V)
-        product(1, 0, 0, 256)
-        store(nc.scalar, 1, 0, 256)
-        product(1, 256, 256, 512)
-        store(nc.sync, 1, 256, 512)
-        product(1, 256, 512, V)
-        store(nc.scalar, 1, 512, V)
+        cast_w(1, 0, 0, P, nc.scalar.copy, 29696)
+        cast_w(1, 0, P, N, nc.scalar.copy, 30720)
+        quantize_w(1, 0, 0, P, 34816)
+        multiply(1, 0, 0)
+        cast_w(1, 1, 0, P, nc.vector.tensor_copy, 31744)
+        quantize_w(1, 1, 0, P, 35328)
+        multiply(1, 1, 0)
+        quantize_w(1, 0, P, N, 31744)
+        multiply(1, 0, 1)
+        cast_w(1, 1, P, N, nc.scalar.copy, 35840)
+        quantize_w(1, 1, P, N, 36864)
+        multiply(1, 1, 1)
+        copy_y0(0, 0, 14848)
+        copy_y0(0, 1, 15872)
+        copy_y0(1, 0, 17408)
+        copy_y0(1, 1, 18432)
+        product(0, 0, 0, 256, nc.sync)
+        product(0, 256, 256, V, nc.sync)
+        product(1, 0, 0, 256, nc.sync)
+        product(1, 256, 256, 512, nc.sync)
+        product(1, 256, 512, V, nc.scalar)

@@ -62,10 +62,10 @@ def tile_picked_pair_lin_mul_sub_p_kernel(tc, x_words, x_scales, w, offs, out):
         nc.vector.tensor_copy(byte_picked[:], byte_table[:].indirect(offsets[:]))
 
         def move_scales(o):
-            for q in range(4):
-                row = ROWS0 + 16 * o + 4 * q
-                nc.sync.dma_start(out=x_plane[QUAD * q + 4 * o:QUAD * q + 4 * o + 4, o * V:o * V + S].bitcast(I32),
-                                  in_=byte_picked[row:row + 4, :].bitcast(I32))
+            for r in range(4):
+                row = ROWS0 + 16 * o + r
+                nc.sync.dma_start(out=x_plane[4 * o + r:P:QUAD, o * V:o * V + S].bitcast(I32),
+                                  in_=byte_picked[row:row + 13:4, :].bitcast(I32))
 
         move_scales(0)
         load_w(0, 1)

@@ -21,8 +21,10 @@ M_TILES = N // P
 QUAD = 32
 ROWS0 = 96
 BANKS = ((0, 256), (256, 640))
-PIECES = {0: ((0, 256),), 256: ((256, 384), (384, 640))}
+PIECES = {(0, 256): ((0, 256),), (256, 640): ((256, 384), (384, 640)), (256, 512): ((256, 384), (384, 512)),
+          (512, 640): ((512, 640),)}
 WALK = 2
+SHARE = 64
 CUT = 1024
 
 
@@ -85,11 +87,17 @@ def tile_picked_pair_lin_mul_sub_p_kernel(tc, x_words, x_scales, w, offs, out):
         w_codes = {}
         w_scales = {}
 
-        def cast_w(d, o, a, b, copy, offset):
+        def new_bf(d, o, a, b, offset):
             w_bf[d, o, a] = shared.tile([P, (b - a) * PACK], BF16, name="w_bf%d%d_%d" % (d, o, a), offset=offset,
                                         align_bytes=64)
-            copy(w_bf[d, o, a][:].rearrange("p (c i j) -> p c j i", i=WALK, j=PACK),
-                 w_raw[d, o][:, :, a:b].rearrange("p j (c i) -> p c j i", i=WALK))
+
+        def cast_part(d, o, a, lo, hi, copy):
+            copy(w_bf[d, o, a][:, (lo - a) * PACK:(hi - a) * PACK].rearrange("p (c i j) -> p c j i", i=WALK, j=PACK),
+                 w_raw[d, o][:, :, lo:hi].rearrange("p j (c i) -> p c j i", i=WALK))
+
+        def cast_w(d, o, a, b, copy, offset):
+            new_bf(d, o, a, b, offset)
+            cast_part(d, o, a, a, b, copy)
 
         def quantize_w(d, o, a, b, offset):
             codes = shared.tile([P, b - a], U32, name="w_codes%d%d_%d" % (d, o, a), offset=offset, align_bytes=64)
@@ -101,14 +109,18 @@ def tile_picked_pair_lin_mul_sub_p_kernel(tc, x_words, x_scales, w, offs, out):
             return codes, scales
 
         acc = {}
+
+        def open_bank(d, mt, a, bank):
+            acc[d, mt, a] = psum.tile([P, 512], F32, name="acc%d%d_%d" % (d, mt, a), offset=2048 * bank)
+
         for d in range(D):
             for mt in range(M_TILES):
-                for a, b in BANKS:
-                    acc[d, mt, a] = psum.tile([P, 512], F32, name="acc%d%d_%d" % (d, mt, a))
+                for i, (a, b) in enumerate(BANKS):
+                    open_bank(d, mt, a, 4 * d + 2 * mt + i)
 
-        def multiply(d, o, mt):
-            for a, b in BANKS:
-                for lo, hi in PIECES[a]:
+        def multiply(d, o, mt, banks=BANKS):
+            for a, b in banks:
+                for lo, hi in PIECES[a, b]:
                     nc.tensor.matmul_mx(out=acc[d, mt, a][:, lo - a:hi - a],
                                         lhsT=w_codes[d, o, mt].bitcast(FP8X4), lhsT_scale=w_scales[d, o, mt],
                                         rhs=x_codes[o, d * V + lo][:, 0:hi - lo].bitcast(FP8X4),
@@ -124,7 +136,7 @@ def tile_picked_pair_lin_mul_sub_p_kernel(tc, x_words, x_scales, w, offs, out):
             nc.scalar.copy(y0[mt, a][:], acc[0, mt, a][:, 0:b - a])
 
         def product(mt, bank, a, b, queue):
-            nc.vector.tensor_tensor(res[mt][:, a:b], acc[1, mt, bank][:, a - bank:b - bank],
+            nc.vector.tensor_tensor(res[mt][:, a:b], acc[1, mt, a][:, 0:b - a],
                                     y0[mt, bank][:, a - bank:b - bank], mybir.AluOpType.mult)
             queue.dma_start(out=out[mt * P:(mt + 1) * P, a:b], in_=res[mt][:, a:b])
 
@@ -148,15 +160,19 @@ def tile_picked_pair_lin_mul_sub_p_kernel(tc, x_words, x_scales, w, offs, out):
         cast_w(1, 0, P, N, nc.scalar.copy, 30720)
         quantize_w(1, 0, 0, P, 34816)
         multiply(1, 0, 0)
-        cast_w(1, 1, 0, P, nc.vector.tensor_copy, 31744)
+        for mt in range(M_TILES):
+            new_bf(1, 1, mt * P, (mt + 1) * P, 31744 + 4096 * mt)
+            cast_part(1, 1, mt * P, mt * P, mt * P + SHARE, nc.vector.tensor_copy)
+            cast_part(1, 1, mt * P, mt * P + SHARE, (mt + 1) * P, nc.scalar.copy)
         quantize_w(1, 1, 0, P, 35328)
         multiply(1, 1, 0)
         quantize_w(1, 0, P, N, 31744)
-        multiply(1, 0, 1)
-        cast_w(1, 1, P, N, nc.scalar.copy, 35840)
         quantize_w(1, 1, P, N, 36864)
-        multiply(1, 1, 1)
         copy_y0(0, 0, 14848)
+        open_bank(1, 1, 512, 0)
+        for bank in ((0, 256), (256, 512), (512, V)):
+            for o in range(PASSES):
+                multiply(1, o, 1, banks=(bank,))
         copy_y0(0, 1, 15872)
         copy_y0(1, 0, 17408)
         copy_y0(1, 1, 18432)

@@ -24,7 +24,7 @@ BANKS = ((0, 256), (256, 640))
 PIECES = {(0, 256): ((0, 256),), (256, 640): ((256, 384), (384, 640)), (256, 512): ((256, 384), (384, 512)),
           (512, 640): ((512, 640),)}
 WALK = 2
-SHARE = 64
+SHARE = 48
 CUT = 1024
 
 
@@ -54,9 +54,9 @@ def tile_picked_pair_lin_mul_sub_p_kernel(tc, x_words, x_scales, w, offs, out):
 
         nc.vector.memset(byte_table[0:ROWS0, :].bitcast(I32), 0)
         nc.gpsimd.memset(x_plane[:].bitcast(I32), 0)
-        nc.sync.dma_start(offsets[:], offs)
         nc.sync.dma_start(out=byte_table[ROWS0:P, :].bitcast(I32),
                           in_=x_scales.rearrange("o r c -> (o r) c").bitcast(I32))
+        nc.sync.dma_start(offsets[:], offs)
         load_words(0)
         load_w(0, 0)
         load_words(1)
@@ -84,28 +84,31 @@ def tile_picked_pair_lin_mul_sub_p_kernel(tc, x_words, x_scales, w, offs, out):
                 x_codes[o, lo] = picked[:, lo - a:]
 
         w_bf = {}
+        place = {}
         w_codes = {}
         w_scales = {}
 
-        def new_bf(d, o, a, b, offset):
-            w_bf[d, o, a] = shared.tile([P, (b - a) * PACK], BF16, name="w_bf%d%d_%d" % (d, o, a), offset=offset,
-                                        align_bytes=64)
+        def stage(name, blocks, offset):
+            w_bf[name] = shared.tile([P, len(blocks) * P * PACK], BF16, name="w_bf_" + name, offset=offset,
+                                     align_bytes=64)
+            for i, block in enumerate(blocks):
+                place[block] = (name, i * P)
 
-        def cast_part(d, o, a, lo, hi, copy):
-            copy(w_bf[d, o, a][:, (lo - a) * PACK:(hi - a) * PACK].rearrange("p (c i j) -> p c j i", i=WALK, j=PACK),
+        def cast(d, o, lo, hi, copy):
+            name, first = place[d, o, lo // P]
+            first = first + lo % P
+            copy(w_bf[name][:, first * PACK:(first + hi - lo) * PACK].rearrange("p (c i j) -> p c j i", i=WALK, j=PACK),
                  w_raw[d, o][:, :, lo:hi].rearrange("p j (c i) -> p c j i", i=WALK))
 
-        def cast_w(d, o, a, b, copy, offset):
-            new_bf(d, o, a, b, offset)
-            cast_part(d, o, a, a, b, copy)
-
-        def quantize_w(d, o, a, b, offset):
-            codes = shared.tile([P, b - a], U32, name="w_codes%d%d_%d" % (d, o, a), offset=offset, align_bytes=64)
-            scales = keep.tile([P, b - a], U8, name="w_scales%d%d_%d" % (d, o, a), align_bytes=64)
-            nc.vector.quantize_mx(out=codes[:].bitcast(FP8X4), scales=scales[:], in_=w_bf[d, o, a][:])
-            for m in range(a, b, P):
-                w_codes[d, o, m // P] = codes[:, m - a:m - a + P]
-                w_scales[d, o, m // P] = scales[:, m - a:m - a + P]
+        def quantize(name, offset):
+            blocks = [block for block in place if place[block][0] == name]
+            codes = shared.tile([P, len(blocks) * P], U32, name="w_codes_" + name, offset=offset, align_bytes=64)
+            scales = keep.tile([P, len(blocks) * P], U8, name="w_scales_" + name, align_bytes=64)
+            nc.vector.quantize_mx(out=codes[:].bitcast(FP8X4), scales=scales[:], in_=w_bf[name][:])
+            for block in blocks:
+                first = place[block][1]
+                w_codes[block] = codes[:, first:first + P]
+                w_scales[block] = scales[:, first:first + P]
             return codes, scales
 
         acc = {}
@@ -141,33 +144,36 @@ def tile_picked_pair_lin_mul_sub_p_kernel(tc, x_words, x_scales, w, offs, out):
             queue.dma_start(out=out[mt * P:(mt + 1) * P, a:b], in_=res[mt][:, a:b])
 
         gather_words(0, 0, S, 20480)
-        cast_w(0, 0, 0, N, nc.scalar.copy, 25600)
-        first_codes, first_scales = quantize_w(0, 0, 0, N, 32768)
+        stage("00", [(0, 0, 0), (0, 0, 1)], 25600)
+        cast(0, 0, 0, N, nc.scalar.copy)
+        first_codes, first_scales = quantize("00", 32768)
         for mt in range(M_TILES):
             nc.tensor.matmul_mx(out=acc[1, mt, 0][:, 0:N],
                                 lhsT=w_codes[0, 0, mt].bitcast(FP8X4), lhsT_scale=w_scales[0, 0, mt],
                                 rhs=first_codes[:].bitcast(FP8X4), rhs_scale=first_scales[:],
                                 start=True, stop=True)
         gather_words(1, 0, CUT, 9216)
-        cast_w(0, 1, 0, N, nc.scalar.copy, 27648)
-        quantize_w(0, 1, 0, N, 33792)
+        stage("01", [(0, 1, 0), (0, 1, 1)], 27648)
+        cast(0, 1, 0, N, nc.scalar.copy)
+        quantize("01", 33792)
         gather_words(1, CUT, S, 0)
         for mt in range(M_TILES):
             multiply(0, 0, mt)
         for mt in range(M_TILES):
             multiply(0, 1, mt)
-        cast_w(1, 0, 0, P, nc.scalar.copy, 29696)
-        cast_w(1, 0, P, N, nc.scalar.copy, 30720)
-        quantize_w(1, 0, 0, P, 34816)
+        stage("10a", [(1, 0, 0)], 29696)
+        stage("11a", [(1, 1, 0)], 30720)
+        stage("1b", [(1, 0, 1), (1, 1, 1)], 36864)
+        cast(1, 0, 0, P, nc.scalar.copy)
+        cast(1, 0, P, N, nc.scalar.copy)
+        quantize("10a", 34816)
         multiply(1, 0, 0)
         for mt in range(M_TILES):
-            new_bf(1, 1, mt * P, (mt + 1) * P, 31744 + 4096 * mt)
-            cast_part(1, 1, mt * P, mt * P, mt * P + SHARE, nc.vector.tensor_copy)
-            cast_part(1, 1, mt * P, mt * P + SHARE, (mt + 1) * P, nc.scalar.copy)
-        quantize_w(1, 1, 0, P, 35328)
+            cast(1, 1, mt * P, mt * P + SHARE, nc.vector.tensor_copy)
+            cast(1, 1, mt * P + SHARE, (mt + 1) * P, nc.scalar.copy)
+        quantize("11a", 35328)
         multiply(1, 1, 0)
-        quantize_w(1, 0, P, N, 31744)
-        quantize_w(1, 1, P, N, 36864)
+        quantize("1b", 35840)
         copy_y0(0, 0, 14848)
         open_bank(1, 1, 512, 0)
         for bank in ((0, 256), (256, 512), (512, V)):

@@ -186,4 +186,4 @@ def tile_picked_pair_lin_mul_sub_p_kernel(tc, x_words, x_scales, w, offs, out):
         product(0, 256, 256, V, nc.sync)
         product(1, 0, 0, 256, nc.sync)
         product(1, 256, 256, 512, nc.sync)
-        product(1, 256, 512, V, nc.scalar)
+        product(1, 256, 512, V, nc.sync)

@@ -17,15 +17,15 @@ P = 128
 PACK = 4
 K_PASS = P * PACK
 PASSES = K // K_PASS
-M_TILES = N // P
 QUAD = 32
 ROWS0 = 96
-BANKS = ((0, 256), (256, 640))
-PIECES = {(0, 256): ((0, 256),), (256, 640): ((256, 384), (384, 640)), (256, 512): ((256, 384), (384, 512)),
-          (512, 640): ((512, 640),)}
+TWO_BANKS = ((0, 256), (256, V))
+THREE_BANKS = ((0, 256), (256, 512), (512, V))
+PIECES = {(0, 256): ((0, 256),), (256, V): ((256, 512), (512, V)), (256, 512): ((256, 512),), (512, V): ((512, V),)}
 WALK = 2
-SHARE = 48
-CUT = 1024
+CUT = V + 256
+SHARE = 56
+KB = 1024
 
 
 def tile_picked_pair_lin_mul_sub_p_kernel(tc, x_words, x_scales, w, offs, out):
@@ -36,32 +36,36 @@ def tile_picked_pair_lin_mul_sub_p_kernel(tc, x_words, x_scales, w, offs, out):
         psum = ctx.enter_context(tc.psum_pool(name="psum", bufs=1))
 
         offsets = keep.tile([P, S // 16], U16, name="offsets")
-        byte_table = shared.tile([P, T], U8, name="byte_table", offset=3072)
+        byte_room = shared.tile([P, 12 * KB], U8, name="byte_room", offset=0)
+        byte_table = byte_room[:, 0:T]
         byte_picked = keep.tile([P, S], U8, name="byte_picked", align_bytes=64)
         x_plane = keep.tile([P, S + V], U8, name="x_plane", align_bytes=64)
         word_table = [keep.tile([P, T], U32, name="word_table%d" % o, align_bytes=64) for o in range(PASSES)]
-        raw_at = {(0, 0): 12288, (0, 1): 0, (1, 0): 4096, (1, 1): 15360}
         w_raw = {}
 
         def load_words(o):
             nc.sync.dma_start(out=word_table[o][:].bitcast(I32),
                               in_=x_words[o].rearrange("p n t -> p (n t)").bitcast(I32))
 
-        def load_w(d, o):
-            w_raw[d, o] = shared.tile([P, PACK, N], F32, name="w_raw%d%d" % (d, o), offset=raw_at[d, o])
-            nc.sync.dma_start(out=w_raw[d, o][:],
-                              in_=w[d, o * K_PASS:(o + 1) * K_PASS, :].rearrange("(p j) m -> p j m", j=PACK))
+        def load_w(d, o, tiles, offset, spare=0):
+            lo, hi = tiles[0] * P, (tiles[-1] + 1) * P
+            room = shared.tile([P, PACK + spare, hi - lo], F32, name="w_raw%d%d%d" % (d, o, tiles[0]), offset=offset)
+            raw = room[:, 0:PACK, :]
+            rows = w[d, o * K_PASS:(o + 1) * K_PASS, :].rearrange("(p j) m -> p j m", j=PACK)
+            nc.sync.dma_start(out=raw, in_=rows[:, :, lo:hi])
+            for mt in tiles:
+                w_raw[d, o, mt] = raw[:, :, mt * P - lo:(mt + 1) * P - lo]
 
-        nc.vector.memset(byte_table[0:ROWS0, :].bitcast(I32), 0)
+        nc.vector.memset(byte_room[0:ROWS0, 0:T].bitcast(I32), 0)
         nc.gpsimd.memset(x_plane[:].bitcast(I32), 0)
-        nc.sync.dma_start(out=byte_table[ROWS0:P, :].bitcast(I32),
+        nc.sync.dma_start(out=byte_room[ROWS0:P, 0:T].bitcast(I32),
                           in_=x_scales.rearrange("o r c -> (o r) c").bitcast(I32))
         nc.sync.dma_start(offsets[:], offs)
         load_words(0)
-        load_w(0, 0)
+        load_w(0, 0, (0, 1), 15 * KB)
         load_words(1)
 
-        nc.vector.tensor_copy(byte_picked[:], byte_table[:].indirect(offsets[:]))
+        nc.vector.tensor_copy(byte_picked[:], byte_table.indirect(offsets[:]))
 
         def move_scales(o):
             for r in range(4):
@@ -70,10 +74,13 @@ def tile_picked_pair_lin_mul_sub_p_kernel(tc, x_words, x_scales, w, offs, out):
                                   in_=byte_picked[row:row + 13:4, :].bitcast(I32))
 
         move_scales(0)
-        load_w(0, 1)
-        load_w(1, 0)
+        load_w(0, 1, (0,), 0)
+        load_w(1, 0, (0,), 2 * KB)
+        load_w(1, 1, (0,), 4 * KB)
         move_scales(1)
-        load_w(1, 1)
+        load_w(0, 1, (1,), 6 * KB)
+        load_w(1, 0, (1,), 8 * KB)
+        load_w(1, 1, (1,), 10 * KB, spare=4)
 
         x_codes = {}
 
@@ -94,11 +101,18 @@ def tile_picked_pair_lin_mul_sub_p_kernel(tc, x_words, x_scales, w, offs, out):
             for i, block in enumerate(blocks):
                 place[block] = (name, i * P)
 
-        def cast(d, o, lo, hi, copy):
-            name, first = place[d, o, lo // P]
-            first = first + lo % P
-            copy(w_bf[name][:, first * PACK:(first + hi - lo) * PACK].rearrange("p (c i j) -> p c j i", i=WALK, j=PACK),
-                 w_raw[d, o][:, :, lo:hi].rearrange("p j (c i) -> p c j i", i=WALK))
+        def columns(block, lo, hi):
+            name, first = place[block]
+            return w_bf[name][:, (first + lo) * PACK:(first + hi) * PACK], w_raw[block][:, :, lo:hi]
+
+        def cast(block, lo=0, hi=P, copy=nc.scalar.copy):
+            grouped, raw = columns(block, lo, hi)
+            copy(grouped.rearrange("p (c i j) -> p c j i", i=WALK, j=PACK), raw.rearrange("p j (c i) -> p c j i", i=WALK))
+
+        def cast_on_gpsimd(block, lo=0, hi=P):
+            grouped, raw = columns(block, lo, hi)
+            nc.gpsimd.tensor_scalar(grouped.rearrange("p (m j) -> p m j", j=PACK), raw.rearrange("p j m -> p m j"),
+                                    1.0, 0.0, mybir.AluOpType.mult, mybir.AluOpType.add)
 
         def quantize(name, offset):
             blocks = [block for block in place if place[block][0] == name]
@@ -109,7 +123,6 @@ def tile_picked_pair_lin_mul_sub_p_kernel(tc, x_words, x_scales, w, offs, out):
                 first = place[block][1]
                 w_codes[block] = codes[:, first:first + P]
                 w_scales[block] = scales[:, first:first + P]
-            return codes, scales
 
         acc = {}
 
@@ -117,11 +130,11 @@ def tile_picked_pair_lin_mul_sub_p_kernel(tc, x_words, x_scales, w, offs, out):
             acc[d, mt, a] = psum.tile([P, 512], F32, name="acc%d%d_%d" % (d, mt, a), offset=2048 * bank)
 
         for d in range(D):
-            for mt in range(M_TILES):
-                for i, (a, b) in enumerate(BANKS):
+            for mt in range(2):
+                for i, (a, b) in enumerate(TWO_BANKS):
                     open_bank(d, mt, a, 4 * d + 2 * mt + i)
 
-        def multiply(d, o, mt, banks=BANKS):
+        def multiply(d, o, mt, banks=TWO_BANKS):
             for a, b in banks:
                 for lo, hi in PIECES[a, b]:
                     nc.tensor.matmul_mx(out=acc[d, mt, a][:, lo - a:hi - a],
@@ -131,59 +144,65 @@ def tile_picked_pair_lin_mul_sub_p_kernel(tc, x_words, x_scales, w, offs, out):
                                         start=(o == 0 and lo == a), stop=(o == PASSES - 1 and hi == b))
 
         y0 = {}
-        res = [keep.tile([P, V], F32, name="res%d" % mt, align_bytes=64) for mt in range(M_TILES)]
 
-        def copy_y0(mt, bank, offset):
-            a, b = BANKS[bank]
-            y0[mt, a] = shared.tile([P, b - a], F32, name="y0_%d_%d" % (mt, a), offset=offset, align_bytes=64)
-            nc.scalar.copy(y0[mt, a][:], acc[0, mt, a][:, 0:b - a])
+        def copy_y0(mt, a, b, offset):
+            bank = 0 if a < 256 else 256
+            copy = shared.tile([P, b - a], F32, name="y0_%d_%d" % (mt, a), offset=offset, align_bytes=64)
+            nc.scalar.copy(copy[:], acc[0, mt, bank][:, a - bank:b - bank])
+            for lo in range(a, b, P):
+                y0[mt, lo] = copy[:, lo - a:]
 
-        def product(mt, bank, a, b, queue):
-            nc.vector.tensor_tensor(res[mt][:, a:b], acc[1, mt, a][:, 0:b - a],
-                                    y0[mt, bank][:, a - bank:b - bank], mybir.AluOpType.mult)
-            queue.dma_start(out=out[mt * P:(mt + 1) * P, a:b], in_=res[mt][:, a:b])
+        def product(mt, bank, a, b, offset):
+            res = shared.tile([P, b - a], F32, name="res%d_%d" % (mt, a), offset=offset, align_bytes=64)
+            nc.vector.tensor_tensor(res[:], acc[1, mt, bank][:, a - bank:b - bank], y0[mt, a][:, 0:b - a],
+                                    mybir.AluOpType.mult)
+            nc.sync.dma_start(out=out[mt * P:(mt + 1) * P, a:b], in_=res[:])
 
-        gather_words(0, 0, S, 20480)
-        stage("00", [(0, 0, 0), (0, 0, 1)], 25600)
-        cast(0, 0, 0, N, nc.scalar.copy)
-        first_codes, first_scales = quantize("00", 32768)
-        for mt in range(M_TILES):
-            nc.tensor.matmul_mx(out=acc[1, mt, 0][:, 0:N],
-                                lhsT=w_codes[0, 0, mt].bitcast(FP8X4), lhsT_scale=w_scales[0, 0, mt],
-                                rhs=first_codes[:].bitcast(FP8X4), rhs_scale=first_scales[:],
-                                start=True, stop=True)
-        gather_words(1, 0, CUT, 9216)
-        stage("01", [(0, 1, 0), (0, 1, 1)], 27648)
-        cast(0, 1, 0, N, nc.scalar.copy)
-        quantize("01", 33792)
-        gather_words(1, CUT, S, 0)
-        for mt in range(M_TILES):
+        gather_words(0, 0, S, 46 * KB)
+        stage("00", [(0, 0, 0), (0, 0, 1)], 21 * KB)
+        cast((0, 0, 0))
+        cast((0, 0, 1))
+        quantize("00", 24 * KB)
+        gather_words(1, 0, V, 15 * KB)
+        for mt in range(2):
             multiply(0, 0, mt)
-        for mt in range(M_TILES):
-            multiply(0, 1, mt)
-        stage("10a", [(1, 0, 0)], 29696)
-        stage("11a", [(1, 1, 0)], 30720)
-        stage("1b", [(1, 0, 1), (1, 1, 1)], 36864)
-        cast(1, 0, 0, P, nc.scalar.copy)
-        cast(1, 0, P, N, nc.scalar.copy)
-        quantize("10a", 34816)
-        multiply(1, 0, 0)
-        for mt in range(M_TILES):
-            cast(1, 1, mt * P, mt * P + SHARE, nc.vector.tensor_copy)
-            cast(1, 1, mt * P + SHARE, (mt + 1) * P, nc.scalar.copy)
-        quantize("11a", 35328)
-        multiply(1, 1, 0)
-        quantize("1b", 35840)
-        copy_y0(0, 0, 14848)
+        stage("01a", [(0, 1, 0)], 26 * KB)
+        cast((0, 1, 0))
+        quantize("01a", 27 * KB)
+        gather_words(1, V, CUT, 0)
+        multiply(0, 1, 0)
+        stage("1a", [(1, 0, 0), (1, 1, 0)], 28 * KB)
+        cast((1, 0, 0))
+        cast_on_gpsimd((1, 1, 0), 0, SHARE)
+        cast((1, 1, 0), SHARE, P)
+        quantize("1a", 30 * KB)
+        gather_words(1, CUT, S, 4 * KB)
+        for o in range(PASSES):
+            multiply(1, o, 0, TWO_BANKS[:1])
+        for o in range(PASSES):
+            multiply(1, o, 0, TWO_BANKS[1:])
+        copy_y0(0, 0, 256, 31 * KB)
+        copy_y0(0, 256, V, 32 * KB)
+        stage("01b", [(0, 1, 1)], 34 * KB)
+        cast_on_gpsimd((0, 1, 1))
+        quantize("01b", 35 * KB)
+        multiply(0, 1, 1)
+        product(0, 0, 0, 256, 6 * KB)
+        stage("10b", [(1, 0, 1)], 27 * KB)
+        cast((1, 0, 1))
+        stage("11b", [(1, 1, 1)], 38 * KB)
+        cast((1, 1, 1), 0, SHARE, nc.vector.tensor_copy)
+        cast((1, 1, 1), SHARE, P)
+        quantize("10b", 10 * KB)
+        quantize("11b", 39 * KB)
+        product(0, 256, 256, V, 13 * KB)
         open_bank(1, 1, 512, 0)
-        for bank in ((0, 256), (256, 512), (512, V)):
-            for o in range(PASSES):
-                multiply(1, o, 1, banks=(bank,))
-        copy_y0(0, 1, 15872)
-        copy_y0(1, 0, 17408)
-        copy_y0(1, 1, 18432)
-        product(0, 0, 0, 256, nc.sync)
-        product(0, 256, 256, V, nc.sync)
-        product(1, 0, 0, 256, nc.sync)
-        product(1, 256, 256, 512, nc.sync)
-        product(1, 256, 512, V, nc.sync)
+        multiply(1, 0, 1, THREE_BANKS[:2])
+        multiply(1, 1, 1, THREE_BANKS[:1])
+        multiply(1, 0, 1, THREE_BANKS[2:])
+        multiply(1, 1, 1, THREE_BANKS[1:])
+        copy_y0(1, 0, 256, 10 * KB + 512)
+        copy_y0(1, 256, 512, 11 * KB + 512)
+        copy_y0(1, 512, V, 12 * KB + 512)
+        for a, b in THREE_BANKS:
+            product(1, a, a, b, 43 * KB + 4 * a)

@@ -24,7 +24,8 @@ THREE_BANKS = ((0, 256), (256, 512), (512, V))
 PIECES = {(0, 256): ((0, 256),), (256, V): ((256, 512), (512, V)), (256, 512): ((256, 512),), (512, V): ((512, V),)}
 WALK = 2
 CUT = V + 256
-SHARE = 56
+SHARE = 64
+GPSIMD_SHARE = 32
 KB = 1024
 
 
@@ -173,8 +174,8 @@ def tile_picked_pair_lin_mul_sub_p_kernel(tc, x_words, x_scales, w, offs, out):
         multiply(0, 1, 0)
         stage("1a", [(1, 0, 0), (1, 1, 0)], 28 * KB)
         cast((1, 0, 0))
-        cast_on_gpsimd((1, 1, 0), 0, SHARE)
-        cast((1, 1, 0), SHARE, P)
+        cast_on_gpsimd((1, 1, 0), 0, GPSIMD_SHARE)
+        cast((1, 1, 0), GPSIMD_SHARE, P)
         quantize("1a", 30 * KB)
         gather_words(1, CUT, S, 4 * KB)
         for o in range(PASSES):
@@ -183,11 +184,11 @@ def tile_picked_pair_lin_mul_sub_p_kernel(tc, x_words, x_scales, w, offs, out):
             multiply(1, o, 0, TWO_BANKS[1:])
         copy_y0(0, 0, 256, 31 * KB)
         copy_y0(0, 256, V, 32 * KB)
+        product(0, 0, 0, 256, 36 * KB)
         stage("01b", [(0, 1, 1)], 34 * KB)
         cast_on_gpsimd((0, 1, 1))
         quantize("01b", 35 * KB)
         multiply(0, 1, 1)
-        product(0, 0, 0, 256, 6 * KB)
         stage("10b", [(1, 0, 1)], 27 * KB)
         cast((1, 0, 1))
         stage("11b", [(1, 1, 1)], 38 * KB)

@@ -24,8 +24,8 @@ THREE_BANKS = ((0, 256), (256, 512), (512, V))
 PIECES = {(0, 256): ((0, 256),), (256, V): ((256, 512), (512, V)), (256, 512): ((256, 512),), (512, V): ((512, V),)}
 WALK = 2
 CUT = V + 256
-SHARE = 64
-GPSIMD_SHARE = 32
+FIRST_SHARE = 32
+LAST_SHARE = 40
 KB = 1024
 
 
@@ -48,10 +48,14 @@ def tile_picked_pair_lin_mul_sub_p_kernel(tc, x_words, x_scales, w, offs, out):
             nc.sync.dma_start(out=word_table[o][:].bitcast(I32),
                               in_=x_words[o].rearrange("p n t -> p (n t)").bitcast(I32))
 
-        def load_w(d, o, tiles, offset, spare=0):
+        rooms = {}
+
+        def load_w(d, o, tiles, offset, spare=0, ahead=0):
             lo, hi = tiles[0] * P, (tiles[-1] + 1) * P
-            room = shared.tile([P, PACK + spare, hi - lo], F32, name="w_raw%d%d%d" % (d, o, tiles[0]), offset=offset)
-            raw = room[:, 0:PACK, :]
+            room = shared.tile([P, (ahead + PACK + spare) * (hi - lo)], F32, name="w_raw%d%d%d" % (d, o, tiles[0]),
+                               offset=offset)
+            rooms[d, o, tiles[0]] = room
+            raw = room[:, ahead * (hi - lo):(ahead + PACK) * (hi - lo)].rearrange("p (j m) -> p j m", j=PACK)
             rows = w[d, o * K_PASS:(o + 1) * K_PASS, :].rearrange("(p j) m -> p j m", j=PACK)
             nc.sync.dma_start(out=raw, in_=rows[:, :, lo:hi])
             for mt in tiles:
@@ -63,7 +67,7 @@ def tile_picked_pair_lin_mul_sub_p_kernel(tc, x_words, x_scales, w, offs, out):
                           in_=x_scales.rearrange("o r c -> (o r) c").bitcast(I32))
         nc.sync.dma_start(offsets[:], offs)
         load_words(0)
-        load_w(0, 0, (0, 1), 15 * KB)
+        load_w(0, 0, (0, 1), 16 * KB)
         load_words(1)
 
         nc.vector.tensor_copy(byte_picked[:], byte_table.indirect(offsets[:]))
@@ -80,8 +84,8 @@ def tile_picked_pair_lin_mul_sub_p_kernel(tc, x_words, x_scales, w, offs, out):
         load_w(1, 1, (0,), 4 * KB)
         move_scales(1)
         load_w(0, 1, (1,), 6 * KB)
-        load_w(1, 0, (1,), 8 * KB)
-        load_w(1, 1, (1,), 10 * KB, spare=4)
+        load_w(1, 0, (1,), 8 * KB, ahead=2)
+        load_w(1, 1, (1,), 11 * KB, spare=4)
 
         x_codes = {}
 
@@ -106,9 +110,10 @@ def tile_picked_pair_lin_mul_sub_p_kernel(tc, x_words, x_scales, w, offs, out):
             name, first = place[block]
             return w_bf[name][:, (first + lo) * PACK:(first + hi) * PACK], w_raw[block][:, :, lo:hi]
 
-        def cast(block, lo=0, hi=P, copy=nc.scalar.copy):
+        def cast(block, lo=0, hi=P):
             grouped, raw = columns(block, lo, hi)
-            copy(grouped.rearrange("p (c i j) -> p c j i", i=WALK, j=PACK), raw.rearrange("p j (c i) -> p c j i", i=WALK))
+            nc.scalar.copy(grouped.rearrange("p (c i j) -> p c j i", i=WALK, j=PACK),
+                           raw.rearrange("p j (c i) -> p c j i", i=WALK))
 
         def cast_on_gpsimd(block, lo=0, hi=P):
             grouped, raw = columns(block, lo, hi)
@@ -119,7 +124,7 @@ def tile_picked_pair_lin_mul_sub_p_kernel(tc, x_words, x_scales, w, offs, out):
             blocks = [block for block in place if place[block][0] == name]
             codes = shared.tile([P, len(blocks) * P], U32, name="w_codes_" + name, offset=offset, align_bytes=64)
             scales = keep.tile([P, len(blocks) * P], U8, name="w_scales_" + name, align_bytes=64)
-            nc.vector.quantize_mx(out=codes[:].bitcast(FP8X4), scales=scales[:], in_=w_bf[name][:])
+            nc.vector.quantize_mx(out=codes[:].bitcast(FP8X4), scales=scales[:], in_=w_bf[name][:, 0:len(blocks) * P * PACK])
             for block in blocks:
                 first = place[block][1]
                 w_codes[block] = codes[:, first:first + P]
@@ -153,29 +158,35 @@ def tile_picked_pair_lin_mul_sub_p_kernel(tc, x_words, x_scales, w, offs, out):
             for lo in range(a, b, P):
                 y0[mt, lo] = copy[:, lo - a:]
 
-        def product(mt, bank, a, b, offset):
-            res = shared.tile([P, b - a], F32, name="res%d_%d" % (mt, a), offset=offset, align_bytes=64)
-            nc.vector.tensor_tensor(res[:], acc[1, mt, bank][:, a - bank:b - bank], y0[mt, a][:, 0:b - a],
+        def product(mt, bank, a, b, res):
+            nc.vector.tensor_tensor(res, acc[1, mt, bank][:, a - bank:b - bank], y0[mt, a][:, 0:b - a],
                                     mybir.AluOpType.mult)
-            nc.sync.dma_start(out=out[mt * P:(mt + 1) * P, a:b], in_=res[:])
+
+        def store(mt, a, b, res):
+            nc.sync.dma_start(out=out[mt * P:(mt + 1) * P, a:b], in_=res)
+
+        def product_and_store(mt, bank, a, b, offset):
+            res = shared.tile([P, b - a], F32, name="res%d_%d" % (mt, a), offset=offset, align_bytes=64)
+            product(mt, bank, a, b, res[:])
+            store(mt, a, b, res[:])
 
         gather_words(0, 0, S, 46 * KB)
         stage("00", [(0, 0, 0), (0, 0, 1)], 21 * KB)
         cast((0, 0, 0))
         cast((0, 0, 1))
         quantize("00", 24 * KB)
-        gather_words(1, 0, V, 15 * KB)
+        gather_words(1, 0, V, 16 * KB)
         for mt in range(2):
             multiply(0, 0, mt)
-        stage("01a", [(0, 1, 0)], 26 * KB)
+        stage("01a", [(0, 1, 0)], 25 * KB)
         cast((0, 1, 0))
         quantize("01a", 27 * KB)
         gather_words(1, V, CUT, 0)
         multiply(0, 1, 0)
-        stage("1a", [(1, 0, 0), (1, 1, 0)], 28 * KB)
+        stage("1a", [(1, 0, 0), (1, 1, 0)], 40 * KB)
         cast((1, 0, 0))
-        cast_on_gpsimd((1, 1, 0), 0, GPSIMD_SHARE)
-        cast((1, 1, 0), GPSIMD_SHARE, P)
+        cast_on_gpsimd((1, 1, 0), 0, FIRST_SHARE)
+        cast((1, 1, 0), FIRST_SHARE, P)
         quantize("1a", 30 * KB)
         gather_words(1, CUT, S, 4 * KB)
         for o in range(PASSES):
@@ -184,26 +195,30 @@ def tile_picked_pair_lin_mul_sub_p_kernel(tc, x_words, x_scales, w, offs, out):
             multiply(1, o, 0, TWO_BANKS[1:])
         copy_y0(0, 0, 256, 31 * KB)
         copy_y0(0, 256, V, 32 * KB)
-        product(0, 0, 0, 256, 36 * KB)
+        product(0, 0, 0, 256, rooms[1, 0, 1][:, 0:256])
         stage("01b", [(0, 1, 1)], 34 * KB)
         cast_on_gpsimd((0, 1, 1))
         quantize("01b", 35 * KB)
         multiply(0, 1, 1)
-        stage("10b", [(1, 0, 1)], 27 * KB)
+        last_stage = shared.tile([P, (2 * P - LAST_SHARE) * PACK], BF16, name="last_stage", offset=26 * KB + 512,
+                                 align_bytes=64)
+        w_bf["10b"] = last_stage[:, 0:P * PACK]
+        place[1, 0, 1] = ("10b", 0)
+        w_bf["11b"] = last_stage[:, (P - LAST_SHARE) * PACK:]
+        place[1, 1, 1] = ("11b", 0)
         cast((1, 0, 1))
-        stage("11b", [(1, 1, 1)], 38 * KB)
-        cast((1, 1, 1), 0, SHARE, nc.vector.tensor_copy)
-        cast((1, 1, 1), SHARE, P)
-        quantize("10b", 10 * KB)
+        quantize("10b", 38 * KB)
+        product(0, 256, 256, 384, rooms[1, 0, 1][:, 256:384])
+        store(0, 0, 384, rooms[1, 0, 1][:, 0:384])
+        cast_on_gpsimd((1, 1, 1), 0, LAST_SHARE)
+        cast((1, 1, 1), LAST_SHARE, P)
         quantize("11b", 39 * KB)
-        product(0, 256, 256, V, 13 * KB)
+        product_and_store(0, 256, 384, V, 14 * KB)
         open_bank(1, 1, 512, 0)
-        multiply(1, 0, 1, THREE_BANKS[:2])
-        multiply(1, 1, 1, THREE_BANKS[:1])
-        multiply(1, 0, 1, THREE_BANKS[2:])
-        multiply(1, 1, 1, THREE_BANKS[1:])
-        copy_y0(1, 0, 256, 10 * KB + 512)
-        copy_y0(1, 256, 512, 11 * KB + 512)
-        copy_y0(1, 512, V, 12 * KB + 512)
+        multiply(1, 0, 1, THREE_BANKS)
+        multiply(1, 1, 1, THREE_BANKS)
+        copy_y0(1, 0, 256, 11 * KB)
+        copy_y0(1, 256, 512, 12 * KB)
+        copy_y0(1, 512, V, 13 * KB)
         for a, b in THREE_BANKS:
-            product(1, a, a, b, 43 * KB + 4 * a)
+            product_and_store(1, a, a, b, 43 * KB + 4 * a)

@@ -24,8 +24,7 @@ THREE_BANKS = ((0, 256), (256, 512), (512, V))
 PIECES = {(0, 256): ((0, 256),), (256, V): ((256, 512), (512, V)), (256, 512): ((256, 512),), (512, V): ((512, V),)}
 WALK = 2
 CUT = V + 256
-FIRST_SHARE = 32
-LAST_SHARE = 40
+GPSIMD_SHARE = 96
 KB = 1024
 
 
@@ -185,8 +184,7 @@ def tile_picked_pair_lin_mul_sub_p_kernel(tc, x_words, x_scales, w, offs, out):
         multiply(0, 1, 0)
         stage("1a", [(1, 0, 0), (1, 1, 0)], 40 * KB)
         cast((1, 0, 0))
-        cast_on_gpsimd((1, 1, 0), 0, FIRST_SHARE)
-        cast((1, 1, 0), FIRST_SHARE, P)
+        cast((1, 1, 0))
         quantize("1a", 30 * KB)
         gather_words(1, CUT, S, 4 * KB)
         for o in range(PASSES):
@@ -197,21 +195,17 @@ def tile_picked_pair_lin_mul_sub_p_kernel(tc, x_words, x_scales, w, offs, out):
         copy_y0(0, 256, V, 32 * KB)
         product(0, 0, 0, 256, rooms[1, 0, 1][:, 0:256])
         stage("01b", [(0, 1, 1)], 34 * KB)
-        cast_on_gpsimd((0, 1, 1))
+        cast_on_gpsimd((0, 1, 1), 0, GPSIMD_SHARE)
+        cast((0, 1, 1), GPSIMD_SHARE, P)
         quantize("01b", 35 * KB)
         multiply(0, 1, 1)
-        last_stage = shared.tile([P, (2 * P - LAST_SHARE) * PACK], BF16, name="last_stage", offset=26 * KB + 512,
-                                 align_bytes=64)
-        w_bf["10b"] = last_stage[:, 0:P * PACK]
-        place[1, 0, 1] = ("10b", 0)
-        w_bf["11b"] = last_stage[:, (P - LAST_SHARE) * PACK:]
-        place[1, 1, 1] = ("11b", 0)
+        stage("10b", [(1, 0, 1)], 27 * KB)
         cast((1, 0, 1))
         quantize("10b", 38 * KB)
         product(0, 256, 256, 384, rooms[1, 0, 1][:, 256:384])
         store(0, 0, 384, rooms[1, 0, 1][:, 0:384])
-        cast_on_gpsimd((1, 1, 1), 0, LAST_SHARE)
-        cast((1, 1, 1), LAST_SHARE, P)
+        stage("11b", [(1, 1, 1)], 28 * KB)
+        cast((1, 1, 1))
         quantize("11b", 39 * KB)
         product_and_store(0, 256, 384, V, 14 * KB)
         open_bank(1, 1, 512, 0)

@@ -128,6 +128,7 @@ def tile_picked_pair_lin_mul_sub_p_kernel(tc, x_words, x_scales, w, offs, out):
                 first = place[block][1]
                 w_codes[block] = codes[:, first:first + P]
                 w_scales[block] = scales[:, first:first + P]
+            return codes, scales
 
         acc = {}
 
@@ -169,12 +170,18 @@ def tile_picked_pair_lin_mul_sub_p_kernel(tc, x_words, x_scales, w, offs, out):
             product(mt, bank, a, b, res[:])
             store(mt, a, b, res[:])
 
-        gather_words(0, 0, S, 46 * KB)
+        gather_words(0, 0, CUT, 46 * KB)
         stage("00", [(0, 0, 0), (0, 0, 1)], 21 * KB)
         cast((0, 0, 0))
         cast((0, 0, 1))
-        quantize("00", 24 * KB)
-        gather_words(1, 0, V, 16 * KB)
+        first_codes, first_scales = quantize("00", 24 * KB)
+        for mt in range(2):
+            nc.tensor.matmul_mx(out=acc[1, mt, 0][:, 0:N],
+                                lhsT=w_codes[0, 0, mt].bitcast(FP8X4), lhsT_scale=w_scales[0, 0, mt],
+                                rhs=first_codes[:].bitcast(FP8X4), rhs_scale=first_scales[:],
+                                start=True, stop=True)
+        gather_words(0, CUT, S, 16 * KB)
+        gather_words(1, 0, V, 17 * KB + 512)
         for mt in range(2):
             multiply(0, 0, mt)
         stage("01a", [(0, 1, 0)], 25 * KB)

@@ -24,7 +24,6 @@ THREE_BANKS = ((0, 256), (256, 512), (512, V))
 PIECES = {(0, 256): ((0, 256),), (256, V): ((256, 512), (512, V)), (256, 512): ((256, 512),), (512, V): ((512, V),)}
 WALK = 2
 CUT = V + 256
-GPSIMD_SHARE = 96
 KB = 1024
 
 
@@ -140,14 +139,14 @@ def tile_picked_pair_lin_mul_sub_p_kernel(tc, x_words, x_scales, w, offs, out):
                 for i, (a, b) in enumerate(TWO_BANKS):
                     open_bank(d, mt, a, 4 * d + 2 * mt + i)
 
-        def multiply(d, o, mt, banks=TWO_BANKS):
+        def multiply(d, o, mt, banks=TWO_BANKS, opening=0):
             for a, b in banks:
                 for lo, hi in PIECES[a, b]:
                     nc.tensor.matmul_mx(out=acc[d, mt, a][:, lo - a:hi - a],
                                         lhsT=w_codes[d, o, mt].bitcast(FP8X4), lhsT_scale=w_scales[d, o, mt],
                                         rhs=x_codes[o, d * V + lo][:, 0:hi - lo].bitcast(FP8X4),
                                         rhs_scale=x_plane[4 * o:P, (o + d) * V + lo:(o + d) * V + hi],
-                                        start=(o == 0 and lo == a), stop=(o == PASSES - 1 and hi == b))
+                                        start=(o == opening and lo == a), stop=(o != opening and hi == b))
 
         y0 = {}
 
@@ -202,8 +201,7 @@ def tile_picked_pair_lin_mul_sub_p_kernel(tc, x_words, x_scales, w, offs, out):
         copy_y0(0, 256, V, 32 * KB)
         product(0, 0, 0, 256, rooms[1, 0, 1][:, 0:256])
         stage("01b", [(0, 1, 1)], 34 * KB)
-        cast_on_gpsimd((0, 1, 1), 0, GPSIMD_SHARE)
-        cast((0, 1, 1), GPSIMD_SHARE, P)
+        cast_on_gpsimd((0, 1, 1))
         quantize("01b", 35 * KB)
         multiply(0, 1, 1)
         stage("10b", [(1, 0, 1)], 27 * KB)
@@ -216,8 +214,11 @@ def tile_picked_pair_lin_mul_sub_p_kernel(tc, x_words, x_scales, w, offs, out):
         quantize("11b", 39 * KB)
         product_and_store(0, 256, 384, V, 14 * KB)
         open_bank(1, 1, 512, 0)
-        multiply(1, 0, 1, THREE_BANKS)
-        multiply(1, 1, 1, THREE_BANKS)
+        multiply(1, 0, 1, THREE_BANKS[:1])
+        multiply(1, 1, 1, THREE_BANKS[:1])
+        for bank in THREE_BANKS[1:]:
+            for o in (1, 0):
+                multiply(1, o, 1, (bank,), opening=1)
         copy_y0(1, 0, 256, 11 * KB)
         copy_y0(1, 256, 512, 12 * KB)
         copy_y0(1, 512, V, 13 * KB)

@@ -82,7 +82,7 @@ def tile_picked_pair_lin_mul_sub_p_kernel(tc, x_words, x_scales, w, offs, out):
         load_w(1, 1, (0,), 4 * KB)
         move_scales(1)
         load_w(0, 1, (1,), 6 * KB)
-        load_w(1, 0, (1,), 8 * KB, ahead=2)
+        load_w(1, 0, (1,), 8 * KB)
         load_w(1, 1, (1,), 11 * KB, spare=4)
 
         x_codes = {}
@@ -199,7 +199,7 @@ def tile_picked_pair_lin_mul_sub_p_kernel(tc, x_words, x_scales, w, offs, out):
             multiply(1, o, 0, TWO_BANKS[1:])
         copy_y0(0, 0, 256, 31 * KB)
         copy_y0(0, 256, V, 32 * KB)
-        product(0, 0, 0, 256, rooms[1, 0, 1][:, 0:256])
+        product_and_store(0, 0, 0, 256, 36 * KB)
         stage("01b", [(0, 1, 1)], 34 * KB)
         cast_on_gpsimd((0, 1, 1))
         quantize("01b", 35 * KB)
@@ -207,12 +207,10 @@ def tile_picked_pair_lin_mul_sub_p_kernel(tc, x_words, x_scales, w, offs, out):
         stage("10b", [(1, 0, 1)], 27 * KB)
         cast((1, 0, 1))
         quantize("10b", 38 * KB)
-        product(0, 256, 256, 384, rooms[1, 0, 1][:, 256:384])
-        store(0, 0, 384, rooms[1, 0, 1][:, 0:384])
         stage("11b", [(1, 1, 1)], 28 * KB)
         cast((1, 1, 1))
         quantize("11b", 39 * KB)
-        product_and_store(0, 256, 384, V, 14 * KB)
+        product_and_store(0, 256, 256, V, 14 * KB)
         open_bank(1, 1, 512, 0)
         multiply(1, 0, 1, THREE_BANKS[:1])
         multiply(1, 1, 1, THREE_BANKS[:1])

@@ -24,6 +24,7 @@ THREE_BANKS = ((0, 256), (256, 512), (512, V))
 PIECES = {(0, 256): ((0, 256),), (256, V): ((256, 512), (512, V)), (256, 512): ((256, 512),), (512, V): ((512, V),)}
 WALK = 2
 CUT = V + 256
+SHARE = 24
 KB = 1024
 
 
@@ -108,10 +109,9 @@ def tile_picked_pair_lin_mul_sub_p_kernel(tc, x_words, x_scales, w, offs, out):
             name, first = place[block]
             return w_bf[name][:, (first + lo) * PACK:(first + hi) * PACK], w_raw[block][:, :, lo:hi]
 
-        def cast(block, lo=0, hi=P):
+        def cast(block, lo=0, hi=P, copy=nc.scalar.copy):
             grouped, raw = columns(block, lo, hi)
-            nc.scalar.copy(grouped.rearrange("p (c i j) -> p c j i", i=WALK, j=PACK),
-                           raw.rearrange("p j (c i) -> p c j i", i=WALK))
+            copy(grouped.rearrange("p (c i j) -> p c j i", i=WALK, j=PACK), raw.rearrange("p j (c i) -> p c j i", i=WALK))
 
         def cast_on_gpsimd(block, lo=0, hi=P):
             grouped, raw = columns(block, lo, hi)
@@ -206,9 +206,10 @@ def tile_picked_pair_lin_mul_sub_p_kernel(tc, x_words, x_scales, w, offs, out):
         multiply(0, 1, 1)
         stage("10b", [(1, 0, 1)], 27 * KB)
         cast((1, 0, 1))
-        quantize("10b", 38 * KB)
         stage("11b", [(1, 1, 1)], 28 * KB)
-        cast((1, 1, 1))
+        cast((1, 1, 1), 0, SHARE, nc.vector.tensor_copy)
+        cast((1, 1, 1), SHARE, P)
+        quantize("10b", 38 * KB)
         quantize("11b", 39 * KB)
         product_and_store(0, 256, 256, V, 14 * KB)
         open_bank(1, 1, 512, 0)

@@ -24,7 +24,7 @@ THREE_BANKS = ((0, 256), (256, 512), (512, V))
 PIECES = {(0, 256): ((0, 256),), (256, V): ((256, 512), (512, V)), (256, 512): ((256, 512),), (512, V): ((512, V),)}
 WALK = 2
 CUT = V + 256
-SHARE = 24
+SHARE = 44
 KB = 1024
 
 
@@ -188,10 +188,12 @@ def tile_picked_pair_lin_mul_sub_p_kernel(tc, x_words, x_scales, w, offs, out):
         quantize("01a", 27 * KB)
         gather_words(1, V, CUT, 0)
         multiply(0, 1, 0)
-        stage("1a", [(1, 0, 0), (1, 1, 0)], 40 * KB)
+        stage("10a", [(1, 0, 0)], 40 * KB)
         cast((1, 0, 0))
+        quantize("10a", 30 * KB)
+        stage("11a", [(1, 1, 0)], 41 * KB)
         cast((1, 1, 0))
-        quantize("1a", 30 * KB)
+        quantize("11a", 30 * KB + 512)
         gather_words(1, CUT, S, 4 * KB)
         for o in range(PASSES):
             multiply(1, o, 0, TWO_BANKS[:1])

@@ -173,12 +173,7 @@ def tile_picked_pair_lin_mul_sub_p_kernel(tc, x_words, x_scales, w, offs, out):
         stage("00", [(0, 0, 0), (0, 0, 1)], 21 * KB)
         cast((0, 0, 0))
         cast((0, 0, 1))
-        first_codes, first_scales = quantize("00", 24 * KB)
-        for mt in range(2):
-            nc.tensor.matmul_mx(out=acc[1, mt, 0][:, 0:N],
-                                lhsT=w_codes[0, 0, mt].bitcast(FP8X4), lhsT_scale=w_scales[0, 0, mt],
-                                rhs=first_codes[:].bitcast(FP8X4), rhs_scale=first_scales[:],
-                                start=True, stop=True)
+        quantize("00", 24 * KB)
         gather_words(0, CUT, S, 16 * KB)
         gather_words(1, 0, V, 17 * KB + 512)
         for mt in range(2):

from contextlib import ExitStack

import concourse.mybir as mybir

K, T, D, S, V, N = 1024, 2048, 2, 1280, 640, 256
FLOPS = 2 * K * N * S + N * V

F32 = mybir.dt.float32
BF16 = mybir.dt.bfloat16
I32 = mybir.dt.int32
U32 = mybir.dt.uint32
U16 = mybir.dt.uint16
U8 = mybir.dt.uint8
FP8X4 = mybir.dt.float8_e4m3fn_x4

P = 128
PACK = 4
K_PASS = P * PACK
PASSES = K // K_PASS
QUAD = 32
ROWS0 = 96
TWO_BANKS = ((0, 256), (256, V))
THREE_BANKS = ((0, 256), (256, 512), (512, V))
PIECES = {(0, 256): ((0, 256),), (256, V): ((256, 512), (512, V)), (256, 512): ((256, 512),), (512, V): ((512, V),)}
WALK = 2
CUT = V + 256
SHARE = 44
KB = 1024


def tile_picked_pair_lin_mul_sub_p_kernel(tc, x_words, x_scales, w, offs, out):
    nc = tc.nc
    with ExitStack() as ctx:
        keep = ctx.enter_context(tc.tile_pool(name="keep", bufs=1))
        shared = ctx.enter_context(tc.tile_pool(name="shared", bufs=1))
        psum = ctx.enter_context(tc.psum_pool(name="psum", bufs=1))

        offsets = keep.tile([P, S // 16], U16, name="offsets")
        byte_room = shared.tile([P, 12 * KB], U8, name="byte_room", offset=0)
        byte_table = byte_room[:, 0:T]
        byte_picked = keep.tile([P, S], U8, name="byte_picked", align_bytes=64)
        x_plane = keep.tile([P, S + V], U8, name="x_plane", align_bytes=64)
        word_table = [keep.tile([P, T], U32, name="word_table%d" % o, align_bytes=64) for o in range(PASSES)]
        w_raw = {}

        def load_words(o):
            nc.sync.dma_start(out=word_table[o][:].bitcast(I32),
                              in_=x_words[o].rearrange("p n t -> p (n t)").bitcast(I32))

        rooms = {}

        def load_w(d, o, tiles, offset, spare=0, ahead=0):
            lo, hi = tiles[0] * P, (tiles[-1] + 1) * P
            room = shared.tile([P, (ahead + PACK + spare) * (hi - lo)], F32, name="w_raw%d%d%d" % (d, o, tiles[0]),
                               offset=offset)
            rooms[d, o, tiles[0]] = room
            raw = room[:, ahead * (hi - lo):(ahead + PACK) * (hi - lo)].rearrange("p (j m) -> p j m", j=PACK)
            rows = w[d, o * K_PASS:(o + 1) * K_PASS, :].rearrange("(p j) m -> p j m", j=PACK)
            nc.sync.dma_start(out=raw, in_=rows[:, :, lo:hi])
            for mt in tiles:
                w_raw[d, o, mt] = raw[:, :, mt * P - lo:(mt + 1) * P - lo]

        nc.vector.memset(byte_room[0:ROWS0, 0:T].bitcast(I32), 0)
        nc.gpsimd.memset(x_plane[:].bitcast(I32), 0)
        nc.sync.dma_start(out=byte_room[ROWS0:P, 0:T].bitcast(I32),
                          in_=x_scales.rearrange("o r c -> (o r) c").bitcast(I32))
        nc.sync.dma_start(offsets[:], offs)
        load_words(0)
        load_w(0, 0, (0, 1), 16 * KB)
        load_words(1)

        nc.vector.tensor_copy(byte_picked[:], byte_table.indirect(offsets[:]))

        def move_scales(o):
            for r in range(4):
                row = ROWS0 + 16 * o + r
                nc.sync.dma_start(out=x_plane[4 * o + r:P:QUAD, o * V:o * V + S].bitcast(I32),
                                  in_=byte_picked[row:row + 13:4, :].bitcast(I32))

        move_scales(0)
        load_w(0, 1, (0,), 0)
        load_w(1, 0, (0,), 2 * KB)
        load_w(1, 1, (0,), 4 * KB)
        move_scales(1)
        load_w(0, 1, (1,), 6 * KB)
        load_w(1, 0, (1,), 8 * KB)
        load_w(1, 1, (1,), 11 * KB, spare=4)

        x_codes = {}

        def gather_words(o, a, b, offset):
            picked = shared.tile([P, b - a], U32, name="x_codes%d_%d" % (o, a), offset=offset, align_bytes=64)
            nc.vector.tensor_copy(picked[:], word_table[o][:].indirect(offsets[:, a // 16:b // 16]))
            for lo in range(a, b, P):
                x_codes[o, lo] = picked[:, lo - a:]

        w_bf = {}
        place = {}
        w_codes = {}
        w_scales = {}

        def stage(name, blocks, offset):
            w_bf[name] = shared.tile([P, len(blocks) * P * PACK], BF16, name="w_bf_" + name, offset=offset,
                                     align_bytes=64)
            for i, block in enumerate(blocks):
                place[block] = (name, i * P)

        def columns(block, lo, hi):
            name, first = place[block]
            return w_bf[name][:, (first + lo) * PACK:(first + hi) * PACK], w_raw[block][:, :, lo:hi]

        def cast(block, lo=0, hi=P, copy=nc.scalar.copy):
            grouped, raw = columns(block, lo, hi)
            copy(grouped.rearrange("p (c i j) -> p c j i", i=WALK, j=PACK), raw.rearrange("p j (c i) -> p c j i", i=WALK))

        def cast_on_gpsimd(block, lo=0, hi=P):
            grouped, raw = columns(block, lo, hi)
            nc.gpsimd.tensor_scalar(grouped.rearrange("p (m j) -> p m j", j=PACK), raw.rearrange("p j m -> p m j"),
                                    1.0, 0.0, mybir.AluOpType.mult, mybir.AluOpType.add)

        def quantize(name, offset):
            blocks = [block for block in place if place[block][0] == name]
            codes = shared.tile([P, len(blocks) * P], U32, name="w_codes_" + name, offset=offset, align_bytes=64)
            scales = keep.tile([P, len(blocks) * P], U8, name="w_scales_" + name, align_bytes=64)
            nc.vector.quantize_mx(out=codes[:].bitcast(FP8X4), scales=scales[:], in_=w_bf[name][:, 0:len(blocks) * P * PACK])
            for block in blocks:
                first = place[block][1]
                w_codes[block] = codes[:, first:first + P]
                w_scales[block] = scales[:, first:first + P]
            return codes, scales

        acc = {}

        def open_bank(d, mt, a, bank):
            acc[d, mt, a] = psum.tile([P, 512], F32, name="acc%d%d_%d" % (d, mt, a), offset=2048 * bank)

        for d in range(D):
            for mt in range(2):
                for i, (a, b) in enumerate(TWO_BANKS):
                    open_bank(d, mt, a, 4 * d + 2 * mt + i)

        def multiply(d, o, mt, banks=TWO_BANKS, opening=0):
            for a, b in banks:
                for lo, hi in PIECES[a, b]:
                    nc.tensor.matmul_mx(out=acc[d, mt, a][:, lo - a:hi - a],
                                        lhsT=w_codes[d, o, mt].bitcast(FP8X4), lhsT_scale=w_scales[d, o, mt],
                                        rhs=x_codes[o, d * V + lo][:, 0:hi - lo].bitcast(FP8X4),
                                        rhs_scale=x_plane[4 * o:P, (o + d) * V + lo:(o + d) * V + hi],
                                        start=(o == opening and lo == a), stop=(o != opening and hi == b))

        y0 = {}

        def copy_y0(mt, a, b, offset):
            bank = 0 if a < 256 else 256
            copy = shared.tile([P, b - a], F32, name="y0_%d_%d" % (mt, a), offset=offset, align_bytes=64)
            nc.scalar.copy(copy[:], acc[0, mt, bank][:, a - bank:b - bank])
            for lo in range(a, b, P):
                y0[mt, lo] = copy[:, lo - a:]

        def product(mt, bank, a, b, res):
            nc.vector.tensor_tensor(res, acc[1, mt, bank][:, a - bank:b - bank], y0[mt, a][:, 0:b - a],
                                    mybir.AluOpType.mult)

        def store(mt, a, b, res):
            nc.sync.dma_start(out=out[mt * P:(mt + 1) * P, a:b], in_=res)

        def product_and_store(mt, bank, a, b, offset):
            res = shared.tile([P, b - a], F32, name="res%d_%d" % (mt, a), offset=offset, align_bytes=64)
            product(mt, bank, a, b, res[:])
            store(mt, a, b, res[:])

        gather_words(0, 0, CUT, 46 * KB)
        stage("00", [(0, 0, 0), (0, 0, 1)], 21 * KB)
        cast((0, 0, 0))
        cast((0, 0, 1))
        quantize("00", 24 * KB)
        gather_words(0, CUT, S, 16 * KB)
        gather_words(1, 0, V, 17 * KB + 512)
        for mt in range(2):
            multiply(0, 0, mt)
        stage("01a", [(0, 1, 0)], 25 * KB)
        cast((0, 1, 0))
        quantize("01a", 27 * KB)
        gather_words(1, V, CUT, 0)
        multiply(0, 1, 0)
        stage("10a", [(1, 0, 0)], 40 * KB)
        cast((1, 0, 0))
        quantize("10a", 30 * KB)
        stage("11a", [(1, 1, 0)], 41 * KB)
        cast((1, 1, 0))
        quantize("11a", 30 * KB + 512)
        gather_words(1, CUT, S, 4 * KB)
        for o in range(PASSES):
            multiply(1, o, 0, TWO_BANKS[:1])
        for o in range(PASSES):
            multiply(1, o, 0, TWO_BANKS[1:])
        copy_y0(0, 0, 256, 31 * KB)
        copy_y0(0, 256, V, 32 * KB)
        product_and_store(0, 0, 0, 256, 36 * KB)
        stage("01b", [(0, 1, 1)], 34 * KB)
        cast_on_gpsimd((0, 1, 1))
        quantize("01b", 35 * KB)
        multiply(0, 1, 1)
        stage("10b", [(1, 0, 1)], 27 * KB)
        cast((1, 0, 1))
        stage("11b", [(1, 1, 1)], 28 * KB)
        cast((1, 1, 1), 0, SHARE, nc.vector.tensor_copy)
        cast((1, 1, 1), SHARE, P)
        quantize("10b", 38 * KB)
        quantize("11b", 39 * KB)
        product_and_store(0, 256, 256, V, 14 * KB)
        open_bank(1, 1, 512, 0)
        multiply(1, 0, 1, THREE_BANKS[:1])
        multiply(1, 1, 1, THREE_BANKS[:1])
        for bank in THREE_BANKS[1:]:
            for o in (1, 0):
                multiply(1, o, 1, (bank,), opening=1)
        copy_y0(1, 0, 256, 11 * KB)
        copy_y0(1, 256, 512, 12 * KB)
        copy_y0(1, 512, V, 13 * KB)
        for a, b in THREE_BANKS:
            product_and_store(1, a, a, b, 43 * KB + 4 * a)
